import numpy as np
import ml_dtypes


def mxq(x, axis, fmt="e4m3"):
    dtype, down = {"e4m3": (ml_dtypes.float8_e4m3fn, 7), "e5m2": (ml_dtypes.float8_e5m2, 14)}[fmt]
    v = np.moveaxis(np.asarray(x, np.float32).astype(ml_dtypes.bfloat16).astype(np.float64), axis, -1)
    blocks = v.reshape(v.shape[:-1] + (-1, 32))
    amax = np.abs(blocks).max(-1, keepdims=True)
    byte = np.maximum(np.where(amax > 0, np.frexp(amax)[1] - 1 + 127, 0) - down, 1)
    scale = np.exp2(byte - 127.0)
    codes = (blocks / scale).astype(np.float32).astype(dtype).astype(np.float64)
    return np.moveaxis((codes * scale).reshape(v.shape), -1, axis)


WIDE = False


def mx_kscale(k):
    if not WIDE:
        return np.ones(k)
    levels = np.array([10, -10, 5, -5, 0])
    if k % 512:
        return np.exp2(np.random.permutation(np.resize(levels, k // 32))).repeat(32)
    a = np.empty((k // 512, 16))
    for p in range(k // 512):
        a[p, :8] = np.random.permutation(np.resize(levels, 8))
        for g in range(8):
            far = levels[np.abs(levels - a[p, g]) >= 10]
            a[p, g + 8] = far[np.random.randint(len(far))]
    return np.exp2(a.ravel()).repeat(32)


def f64(x):
    return np.asarray(x).astype(np.float64)


def striped(idx):
    return np.tile(idx.reshape(-1, 16).T, (8, 1)).astype(np.uint16)


def unstriped(offs):
    return offs[:16].T.reshape(-1).astype(np.int64)


E2M1 = np.array([0.0, 0.5, 1.0, 1.5, 2.0, 3.0, 4.0, 6.0, -0.0, -0.5, -1.0, -1.5, -2.0, -3.0, -4.0, -6.0])


def pack_weight(w, fmt):
    k, n = w.shape
    w = f64(np.asarray(w, np.float32).astype(ml_dtypes.bfloat16)).reshape(k // 32, 32, n)
    amax = np.abs(w).max(1)
    if fmt == "e4m3":
        byte = np.frexp(amax)[1] - 1 + 127 - 7
    else:
        mant, ex = np.frexp(amax / 6.0)
        byte = np.where(mant > 0.5, ex, ex - 1) + 127
    byte = np.clip(np.where(amax > 0, byte, 1), 1, 254)
    scaled = (w * np.exp2(127.0 - byte)[:, None, :]).reshape(k, n).astype(np.float32)
    by_word = np.ascontiguousarray(scaled.reshape(k // 512, 128, 4, n).transpose(0, 1, 3, 2))
    if fmt == "e4m3":
        words = by_word.astype(ml_dtypes.float8_e4m3fn).view(np.uint8)
    else:
        c = by_word.astype(ml_dtypes.float4_e2m1fn).view(np.uint8) & 0xF
        words = (c[..., 0::2] | (c[..., 1::2] << 4)).reshape(k // 512, 128, 2 * n)
    return np.ascontiguousarray(words), np.ascontiguousarray(byte.astype(np.uint8).reshape(k // 512, 16, n))


def unpack_weight(words, scales, fmt):
    g, _, n = scales.shape
    words = np.ascontiguousarray(words).reshape(g, 128, n, -1)
    if fmt == "e4m3":
        vals = words.view(ml_dtypes.float8_e4m3fn).astype(np.float64)
    else:
        nib = np.empty((g, 128, n, 4), np.uint8)
        nib[..., 0::2] = words & 0xF
        nib[..., 1::2] = words >> 4
        vals = E2M1[nib]
    vals = vals * np.repeat(np.exp2(scales.astype(np.float64) - 127.0), 8, axis=1)[..., None]
    return vals.transpose(0, 1, 3, 2).reshape(g * 512, n)


def gelu(v):
    return 0.5 * v * (1.0 + np.tanh(np.sqrt(2.0 / np.pi) * (v + 0.044715 * v**3)))


K, H, N, T, S, T2, P = 1024, 1024, 512, 2048, 1024, 2048, 1024


def setup_inputs():
    n = np.random.standard_normal
    s = mx_kscale(K)[:, None]
    u = mx_kscale(H)[:, None]
    tab_words, tab_scales = pack_weight(n((K, T)) * s, "e4m3")
    w1_words, w1_scales = pack_weight(0.8 * n((K, H)) / np.sqrt(K) / s, "e2m1")
    w3_words, w3_scales = pack_weight(n((H, N)) / np.sqrt(H) / u, "e4m3")
    return {
        "tab_words": tab_words, "tab_scales": tab_scales,
        "offs": striped(np.random.permutation(T)[:S]),
        "w1_words": w1_words, "w1_scales": w1_scales,
        "xn": (n((K, S)) * np.sqrt(s)).astype(np.float32),
        "w2": (0.4 * n((K, H)) / np.sqrt(K) / s).astype(np.float32),
        "wgs": np.exp(0.3 * n((128, S))).astype(np.float32),
        "offs2": striped(np.random.permutation(T2)[:S]),
        "offs3": striped(np.random.permutation(T2)[:P]),
        "gain": (np.exp(0.3 * n(H)) * u[:, 0]).astype(np.float32),
        "disp": (0.7 * n((H, P)) * u).astype(np.float32),
        "w3_words": w3_words, "w3_scales": w3_scales,
    }


def reference(tab_words, tab_scales, offs, w1_words, w1_scales, xn, w2, wgs,
              offs2, offs3, gain, disp, w3_words, w3_scales):
    v = unpack_weight(tab_words, tab_scales, "e4m3")[:, unstriped(offs)]
    w1 = unpack_weight(w1_words, w1_scales, "e2m1")
    sq = mxq(np.square(f64(xn)), 0, "e4m3")
    h = np.tanh(w1.T @ v + mxq(f64(w2), 0, "e4m3").T @ sq)
    page = np.zeros((H, T2))
    page[:, unstriped(offs2)] = np.tile(f64(wgs), (H // 128, 1)) * h
    x = page[:, unstriped(offs3)]
    d = f64(disp)
    z = x * (f64(gain)[:, None] + d) + d
    w3 = unpack_weight(w3_words, w3_scales, "e4m3")
    return w3.T @ mxq(z, 0, "e4m3")

@@ -1,0 +1,290 @@
+from contextlib import ExitStack
+
+import concourse.mybir as mybir
+from concourse.masks import make_identity
+
+K, H, N, T, S, T2, M = 1024, 1024, 512, 2048, 1024, 2048, 1024
+FLOPS = 2 * (2 * K * H * S + H * N * M)
+
+F32 = mybir.dt.float32
+BF16 = mybir.dt.bfloat16
+I32 = mybir.dt.int32
+U32 = mybir.dt.uint32
+U16 = mybir.dt.uint16
+U8 = mybir.dt.uint8
+FP8X4 = mybir.dt.float8_e4m3fn_x4
+FP4X4 = mybir.dt.float4_e2m1fn_x4
+ACT = mybir.ActivationFunctionType
+MULT = mybir.AluOpType.mult
+
+P = 128
+PACK = 4
+K_PASS = P * PACK
+PASSES = K // K_PASS
+BANK = 512
+PIECE = 256
+ROW_TILES = H // P
+PER_COL = 16
+
+
+def tile_list_fibre_nonlinear_deinterleave_kernel(
+    tc, tab_words, tab_scales, offs, w1_words, w1_scales, xn, w2, wgs, offs2, offs3, gain, disp, w3_words, w3_scales, out
+):
+    nc = tc.nc
+    with ExitStack() as ctx:
+        keep = ctx.enter_context(tc.tile_pool(name="keep", bufs=1))
+        ring = ctx.enter_context(tc.tile_pool(name="ring", bufs=2))
+        psum = ctx.enter_context(tc.psum_pool(name="psum", bufs=2))
+
+        def held(shape, dtype, name):
+            return keep.tile(shape, dtype, name=name, align_bytes=64)
+
+        idx1 = held([P, S // PER_COL], U16, "idx1")
+        idx2 = held([P, S // PER_COL], U16, "idx2")
+        idx3 = held([P, M // PER_COL], U16, "idx3")
+        tab_w = [held([P, T], I32, f"tab_w{a}") for a in range(PASSES)]
+        tab_s = held([P, PASSES, T], U8, "tab_s")
+        v_w = [held([P, S], U32, f"v_w{a}") for a in range(PASSES)]
+        v_s = [held([P, S], U8, f"v_s{a}") for a in range(PASSES)]
+        w1_head = held([P, PASSES, 2 * PIECE], U8, "w1_head")
+        w1_rest = held([P, PASSES, 2 * (H - PIECE)], U8, "w1_rest")
+        w1_s = held([P, PASSES, H], U8, "w1_s")
+        w3_w = held([P, PASSES, N], I32, "w3_w")
+        w3_s = held([P, PASSES, N], U8, "w3_s")
+        sq_w = [held([P, S], U32, f"sq_w{a}") for a in range(PASSES)]
+        sq_s = [held([P, S], U8, f"sq_s{a}") for a in range(PASSES)]
+        w2_w = [held([P, H], U32, f"w2_w{a}") for a in range(PASSES)]
+        w2_s = [held([P, H], U8, f"w2_s{a}") for a in range(PASSES)]
+        z_w = [held([P, M], U32, f"z_w{a}") for a in range(PASSES)]
+        z_s = [held([P, M], U8, f"z_s{a}") for a in range(PASSES)]
+        weights = held([P, S], F32, "weights")
+        pages = [held([P, T2], F32, f"page{i}") for i in range(2)]
+        ident = held([P, P], F32, "ident")
+        gain_rows = held([P, P], F32, "gain_rows")
+        gain_col = held([P, ROW_TILES], F32, "gain_col")
+        warm = held([P, 2], F32, "warm")
+
+        nc.vector.memset(tab_s[:].rearrange("p a t -> p (a t)").bitcast(I32), 0)
+        nc.vector.memset(w1_s[:].rearrange("p a t -> p (a t)").bitcast(I32), 0)
+        nc.vector.memset(w3_s[:].rearrange("p a t -> p (a t)").bitcast(I32), 0)
+        for page in pages:
+            nc.vector.memset(page[:], 0.0)
+        nc.gpsimd.memset(warm[:], 0.0)
+        nc.scalar.activation(warm[:, 1:2], warm[:, 0:1], ACT.Tanh)
+        make_identity(nc, ident[:])
+        nc.gpsimd.memset(gain_rows[:], 0.0)
+
+        def load_scale_rows(plane, scales):
+            for q in range(4):
+                nc.sync.dma_start(
+                    plane[32 * q : 32 * q + 4, :, :].bitcast(I32),
+                    scales[:, 4 * q : 4 * q + 4, :].rearrange("a r n -> r a n").bitcast(I32),
+                )
+
+        def load_table_words(a):
+            nc.sync.dma_start(tab_w[a][:], tab_words[a].rearrange("p t i -> p (t i)").bitcast(I32))
+
+        def load_rows(matrix, a, piece):
+            raw = ring.tile([P, PACK, PIECE], F32, name="raw", tag="raw", bufs=14, align_bytes=64)
+            rows = matrix[a * K_PASS : (a + 1) * K_PASS, piece * PIECE : (piece + 1) * PIECE]
+            nc.sync.dma_start(raw[:], rows.rearrange("(p t) w -> p t w", t=PACK))
+            return raw
+
+        def load_disp(c):
+            raw = ring.tile([P, M], F32, name="raw", tag="raw", bufs=14, align_bytes=64)
+            nc.sync.dma_start(raw[:], disp[c * P : (c + 1) * P, :])
+            return raw
+
+        w1_bytes = w1_words.rearrange("a p n -> p a n")
+        xn_raw, w2_raw, d = {}, {}, {}
+        load_table_words(0)
+        nc.sync.dma_start(idx1[:], offs)
+        nc.sync.dma_start(idx2[:], offs2)
+        load_scale_rows(tab_s, tab_scales)
+        for a in range(PASSES):
+            xn_raw[a, 0] = load_rows(xn, a, 0)
+        for a in range(PASSES):
+            w2_raw[a, 0] = load_rows(w2, a, 0)
+        load_scale_rows(w1_s, w1_scales)
+        nc.sync.dma_start(w1_head[:].bitcast(I32), w1_bytes[:, :, : 2 * PIECE].bitcast(I32))
+        nc.sync.dma_start(weights[:, :PIECE], wgs[:, :PIECE])
+        load_table_words(1)
+        for a in range(PASSES):
+            xn_raw[a, 1] = load_rows(xn, a, 1)
+        nc.sync.dma_start(weights[:, PIECE:], wgs[:, PIECE:])
+        for piece in (2, 3):
+            for a in range(PASSES):
+                xn_raw[a, piece] = load_rows(xn, a, piece)
+        nc.sync.dma_start(w1_rest[:].bitcast(I32), w1_bytes[:, :, 2 * PIECE :].bitcast(I32))
+        for a in range(PASSES):
+            w2_raw[a, 1] = load_rows(w2, a, 1)
+        nc.sync.dma_start(idx3[:], offs3)
+        nc.sync.dma_start(gain_rows[:ROW_TILES, :], gain.rearrange("(c p) -> c p", p=P))
+        for piece in range(1, 4):
+            for c in (2 * piece - 2, 2 * piece - 1):
+                d[c] = load_disp(c)
+            if piece < 3:
+                for a in range(PASSES):
+                    w2_raw[a, piece + 1] = load_rows(w2, a, piece + 1)
+        for c in (6, 7):
+            d[c] = load_disp(c)
+        nc.sync.dma_start(w3_w[:], w3_words.rearrange("a p n i -> p a (n i)").bitcast(I32))
+        load_scale_rows(w3_s, w3_scales)
+
+        def quantise_rows(raw, func, codes, scales, piece):
+            grouped = ring.tile([P, PIECE, PACK], BF16, name="grouped", bufs=3, align_bytes=64)
+            nc.scalar.activation(
+                grouped[:].rearrange("p (c i) t -> p c t i", i=4),
+                raw[:].rearrange("p t (c i) -> p c t i", i=4),
+                func,
+            )
+            cols = slice(piece * PIECE, (piece + 1) * PIECE)
+            nc.vector.quantize_mx(codes[:, cols].bitcast(FP8X4), scales[:, cols], grouped[:].rearrange("p w t -> p (w t)"))
+
+        def quantise_sq(piece):
+            for a in range(PASSES):
+                quantise_rows(xn_raw[a, piece], ACT.Square, sq_w[a], sq_s[a], piece)
+
+        def quantise_w2(piece):
+            for a in range(PASSES):
+                quantise_rows(w2_raw[a, piece], ACT.Copy, w2_w[a], w2_s[a], piece)
+
+        def entries(idx, first, count):
+            return idx[:, first // PER_COL : (first + count) // PER_COL]
+
+        def gather_words(a, first, count):
+            nc.vector.tensor_copy(v_w[a][:, first : first + count], tab_w[a][:].bitcast(U32).indirect(entries(idx1, first, count)))
+
+        def scatter_h(c, first, count):
+            acc = psum.tile([P, BANK], F32, name="acc", tag="acc", bufs=4)
+            rows = slice(c * P, (c + 1) * P)
+            cols = slice(first, first + count)
+            for a in range(PASSES):
+                nc.tensor.matmul_mx(
+                    acc[:, :count], w2_w[a][:, rows].bitcast(FP8X4), w2_s[a][:, rows],
+                    sq_w[a][:, cols].bitcast(FP8X4), sq_s[a][:, cols], start=(a == 0), stop=False,
+                )
+            width = BANK if count == BANK else P
+            w1_tile, w1_first = (w1_head, c * P) if c * P < PIECE else (w1_rest, c * P - PIECE)
+            for a in range(PASSES):
+                for lo in range(0, count, width):
+                    part = slice(first + lo, first + lo + width)
+                    nc.tensor.matmul_mx(
+                        acc[:, lo : lo + width], w1_tile[:, a, 2 * w1_first : 2 * (w1_first + P)].bitcast(FP4X4), w1_s[:, a, rows],
+                        v_w[a][:, part].bitcast(FP8X4), v_s[a][:, part],
+                        start=False, stop=(a == PASSES - 1 and lo + width == count),
+                    )
+            h = ring.tile([P, BANK], F32, name="h", bufs=6, align_bytes=64)
+            nc.scalar.activation(h[:, :count], acc[:, :count], ACT.Tanh)
+            nc.vector.tensor_tensor(pages[c % 2][:].indirect(entries(idx2, first, count)), h[:, :count], weights[:, cols], MULT)
+
+        def gain_plus_disp(c):
+            gd = ring.tile([P, M], F32, name="gd", bufs=2, align_bytes=64)
+            nc.scalar.activation(gd[:], d[c][:], ACT.Identity, bias=gain_col[:, c : c + 1], scale=1.0)
+            return gd
+
+        def z_rows(c, gd, zt, first, count, step):
+            y = ring.tile([P, M], F32, name="y", bufs=2, align_bytes=64)
+            nc.vector.tensor_tensor(
+                y[:, :count], pages[c % 2][:].indirect(entries(idx3, first, count)), gd[:, first : first + count], MULT
+            )
+            for lo in range(0, count, step):
+                blocks = step // P
+                bank = psum.tile([P, BANK], F32, name="zt_bank", bufs=2)
+                for src, off, is_last in ((d[c], first + lo, False), (y, lo, True)):
+                    for k in range(blocks):
+                        nc.tensor.matmul(
+                            bank[:, k * P : (k + 1) * P], src[:, off + k * P : off + (k + 1) * P], ident[:],
+                            is_transpose=True, start=(k == 0 and not is_last), stop=(is_last and k == blocks - 1),
+                        )
+                quarter = c % PACK
+                for part in range(0, step, PIECE):
+                    nc.scalar.copy(
+                        zt[(first + lo + part) // PIECE][:, :, :, 32 * quarter : 32 * (quarter + 1), :],
+                        bank[:, part : part + PIECE].rearrange("m (k p u e) -> m k u p e", k=2, u=2, e=2),
+                    )
+
+        def quantise_z(a, zt, first, count):
+            words = ring.tile([P, BANK, 2], F32, name="z_words", bufs=2, align_bytes=64)
+            for lo in range(0, count, PIECE):
+                bank = psum.tile([P, 2, 2, P], F32, name="zb_bank", bufs=2)
+                for k in range(2):
+                    for u in range(2):
+                        nc.tensor.transpose(
+                            bank[:, k, u, :], zt[(first + lo) // PIECE][:, k, u, :, :].rearrange("m p e -> m (p e)").bitcast(F32), ident[:]
+                        )
+                nc.scalar.copy(
+                    words[:, lo : lo + PIECE, :].rearrange("p (k m) u -> p k m u", k=2),
+                    bank[:].rearrange("p k u m -> p k m u"),
+                )
+            cols = slice(first, first + count)
+            nc.vector.quantize_mx(
+                z_w[a][:, cols].bitcast(FP8X4), z_s[a][:, cols],
+                words[:, :count, :].rearrange("p m u -> p (m u)").bitcast(BF16),
+            )
+
+        def out_piece(first):
+            cols = slice(first, first + PIECE)
+            staged = ring.tile([P, N // P, PIECE], F32, name="staged", bufs=3, align_bytes=64)
+            for half in range(2):
+                acc = psum.tile([P, BANK], F32, name="acc", tag="acc", bufs=4)
+                for a in range(PASSES):
+                    for k in range(2):
+                        n0 = (2 * half + k) * P
+                        nc.tensor.matmul_mx(
+                            acc[:, k * PIECE : (k + 1) * PIECE],
+                            w3_w[:, a, n0 : n0 + P].bitcast(FP8X4), w3_s[:, a, n0 : n0 + P],
+                            z_w[a][:, cols].bitcast(FP8X4), z_s[a][:, cols],
+                            start=(a == 0 and k == 0), stop=(a == PASSES - 1 and k == 1),
+                        )
+                dst = staged[:, 2 * half : 2 * half + 2, :].rearrange("p k m -> p (k m)")
+                if half == 0:
+                    nc.scalar.copy(dst, acc[:])
+                else:
+                    nc.vector.tensor_copy(dst, acc[:])
+            nc.sync.dma_start(out[:, cols].rearrange("(k p) m -> p k m", p=P), staged[:])
+
+        gather_words(0, 0, S)
+        for a in range(PASSES):
+            nc.vector.tensor_copy(v_s[a][:], tab_s[:, a, :].indirect(idx1[:]))
+        quantise_sq(0)
+        quantise_w2(0)
+        gather_words(1, 0, PIECE)
+        for piece in range(4):
+            if piece > 0:
+                quantise_sq(piece)
+            for c in range(2):
+                scatter_h(c, piece * PIECE, PIECE)
+                if piece == 0 and c == 0:
+                    gather_words(1, PIECE, S - PIECE)
+        quantise_w2(1)
+
+        gain_bank = psum.tile([P, 2, 2, P], F32, name="zb_bank", bufs=2)
+        nc.tensor.transpose(gain_bank[:, 0, 0, :], gain_rows[:], ident[:])
+        nc.scalar.copy(gain_col[:], gain_bank[:, 0, 0, :ROW_TILES])
+
+        def new_zt():
+            return [ring.tile([P, 2, 2, P, 2], BF16, name="zt", bufs=M // PIECE, align_bytes=64) for piece in range(M // PIECE)]
+
+        zt = new_zt()
+        z_rows(0, gain_plus_disp(0), zt, 0, M, BANK)
+        for c in range(1, ROW_TILES - 1):
+            if c in (2, 4):
+                quantise_w2(c // 2 + 1)
+            if c > 1:
+                scatter_h(c, BANK, BANK)
+            scatter_h(c + 1, 0, BANK)
+            if c == PACK:
+                zt = new_zt()
+            z_rows(c, gain_plus_disp(c), zt, 0, M, BANK)
+            if c == PACK - 1:
+                for first in range(0, M, BANK):
+                    quantise_z(0, zt, first, BANK)
+        last = ROW_TILES - 1
+        scatter_h(last, BANK, BANK)
+        gd = gain_plus_disp(last)
+        for first in range(0, M, PIECE):
+            z_rows(last, gd, zt, first, PIECE, PIECE)
+        for first in range(0, M, PIECE):
+            quantise_z(1, zt, first, PIECE)
+            out_piece(first)

@@ -25,6 +25,7 @@ BANK = 512
 PIECE = 256
 ROW_TILES = H // P
 PER_COL = 16
+TAIL_PARTS = [(0, 256), (256, 256), (512, 256), (768, 128), (896, 128)]
 
 
 def tile_list_fibre_nonlinear_deinterleave_kernel(
@@ -34,7 +35,10 @@ def tile_list_fibre_nonlinear_deinterleave_kernel(
     with ExitStack() as ctx:
         keep = ctx.enter_context(tc.tile_pool(name="keep", bufs=1))
         ring = ctx.enter_context(tc.tile_pool(name="ring", bufs=2))
-        psum = ctx.enter_context(tc.psum_pool(name="psum", bufs=2))
+        psum = ctx.enter_context(tc.psum_pool(name="psum", bufs=1))
+
+        def bank_tile(number):
+            return psum.tile([P, BANK], F32, name=f"bank{number}")
 
         def held(shape, dtype, name):
             return keep.tile(shape, dtype, name=name, align_bytes=64)
@@ -53,8 +57,8 @@ def tile_list_fibre_nonlinear_deinterleave_kernel(
         w3_s = held([P, PASSES, N], U8, "w3_s")
         sq_w = [held([P, S], U32, f"sq_w{a}") for a in range(PASSES)]
         sq_s = [held([P, S], U8, f"sq_s{a}") for a in range(PASSES)]
-        w2_w = [held([P, H], U32, f"w2_w{a}") for a in range(PASSES)]
-        w2_s = [held([P, H], U8, f"w2_s{a}") for a in range(PASSES)]
+        w2_w = [held([P, PASSES, PIECE], U32, f"w2_w{piece}") for piece in range(H // PIECE)]
+        w2_s = [held([P, PASSES, PIECE], U8, f"w2_s{piece}") for piece in range(H // PIECE)]
         z_w = [held([P, M], U32, f"z_w{a}") for a in range(PASSES)]
         z_s = [held([P, M], U8, f"z_s{a}") for a in range(PASSES)]
         weights = held([P, S], F32, "weights")
@@ -66,17 +70,17 @@ def tile_list_fibre_nonlinear_deinterleave_kernel(
 
         nc.vector.memset(tab_s[:].rearrange("p a t -> p (a t)").bitcast(I32), 0)
         nc.vector.memset(w1_s[:].rearrange("p a t -> p (a t)").bitcast(I32), 0)
-        nc.vector.memset(w3_s[:].rearrange("p a t -> p (a t)").bitcast(I32), 0)
-        for page in pages:
-            nc.vector.memset(page[:], 0.0)
+        nc.vector.memset(pages[0][:], 0.0)
         nc.gpsimd.memset(warm[:], 0.0)
+        nc.gpsimd.memset(pages[1][:], 0.0)
+        nc.gpsimd.memset(w3_s[:].rearrange("p a t -> p (a t)").bitcast(I32), 0)
         nc.scalar.activation(warm[:, 1:2], warm[:, 0:1], ACT.Tanh)
         make_identity(nc, ident[:])
         nc.gpsimd.memset(gain_rows[:], 0.0)
 
-        def load_scale_rows(plane, scales):
+        def load_scale_rows(queue, plane, scales):
             for q in range(4):
-                nc.sync.dma_start(
+                queue.dma_start(
                     plane[32 * q : 32 * q + 4, :, :].bitcast(I32),
                     scales[:, 4 * q : 4 * q + 4, :].rearrange("a r n -> r a n").bitcast(I32),
                 )
@@ -97,18 +101,19 @@ def tile_list_fibre_nonlinear_deinterleave_kernel(
 
         w1_bytes = w1_words.rearrange("a p n -> p a n")
         xn_raw, w2_raw, d = {}, {}, {}
-        load_table_words(0)
         nc.sync.dma_start(idx1[:], offs)
         nc.sync.dma_start(idx2[:], offs2)
-        load_scale_rows(tab_s, tab_scales)
+        nc.sync.dma_start(idx3[:], offs3)
+        nc.sync.dma_start(weights[:, :PIECE], wgs[:, :PIECE])
+        load_table_words(0)
+        load_scale_rows(nc.scalar, tab_s, tab_scales)
         for a in range(PASSES):
             xn_raw[a, 0] = load_rows(xn, a, 0)
         for a in range(PASSES):
             w2_raw[a, 0] = load_rows(w2, a, 0)
-        load_scale_rows(w1_s, w1_scales)
-        nc.sync.dma_start(w1_head[:].bitcast(I32), w1_bytes[:, :, : 2 * PIECE].bitcast(I32))
-        nc.sync.dma_start(weights[:, :PIECE], wgs[:, :PIECE])
         load_table_words(1)
+        load_scale_rows(nc.sync, w1_s, w1_scales)
+        nc.sync.dma_start(w1_head[:].bitcast(I32), w1_bytes[:, :, : 2 * PIECE].bitcast(I32))
         for a in range(PASSES):
             xn_raw[a, 1] = load_rows(xn, a, 1)
         nc.sync.dma_start(weights[:, PIECE:], wgs[:, PIECE:])
@@ -118,7 +123,6 @@ def tile_list_fibre_nonlinear_deinterleave_kernel(
         nc.sync.dma_start(w1_rest[:].bitcast(I32), w1_bytes[:, :, 2 * PIECE :].bitcast(I32))
         for a in range(PASSES):
             w2_raw[a, 1] = load_rows(w2, a, 1)
-        nc.sync.dma_start(idx3[:], offs3)
         nc.sync.dma_start(gain_rows[:ROW_TILES, :], gain.rearrange("(c p) -> c p", p=P))
         for piece in range(1, 4):
             for c in (2 * piece - 2, 2 * piece - 1):
@@ -129,25 +133,29 @@ def tile_list_fibre_nonlinear_deinterleave_kernel(
         for c in (6, 7):
             d[c] = load_disp(c)
         nc.sync.dma_start(w3_w[:], w3_words.rearrange("a p n i -> p a (n i)").bitcast(I32))
-        load_scale_rows(w3_s, w3_scales)
+        load_scale_rows(nc.sync, w3_s, w3_scales)
 
-        def quantise_rows(raw, func, codes, scales, piece):
-            grouped = ring.tile([P, PIECE, PACK], BF16, name="grouped", bufs=3, align_bytes=64)
+        def interleave(grouped, raw, func):
             nc.scalar.activation(
-                grouped[:].rearrange("p (c i) t -> p c t i", i=4),
-                raw[:].rearrange("p t (c i) -> p c t i", i=4),
-                func,
+                grouped.rearrange("p (c i) t -> p c t i", i=4), raw[:].rearrange("p t (c i) -> p c t i", i=4), func
             )
-            cols = slice(piece * PIECE, (piece + 1) * PIECE)
-            nc.vector.quantize_mx(codes[:, cols].bitcast(FP8X4), scales[:, cols], grouped[:].rearrange("p w t -> p (w t)"))
 
         def quantise_sq(piece):
+            cols = slice(piece * PIECE, (piece + 1) * PIECE)
             for a in range(PASSES):
-                quantise_rows(xn_raw[a, piece], ACT.Square, sq_w[a], sq_s[a], piece)
+                grouped = ring.tile([P, PIECE, PACK], BF16, name="sq_grouped", bufs=3, align_bytes=64)
+                interleave(grouped[:], xn_raw[a, piece], ACT.Square)
+                nc.vector.quantize_mx(sq_w[a][:, cols].bitcast(FP8X4), sq_s[a][:, cols], grouped[:].rearrange("p w t -> p (w t)"))
 
         def quantise_w2(piece):
+            grouped = ring.tile([P, PASSES, PIECE, PACK], BF16, name="w2_grouped", bufs=1, align_bytes=64)
             for a in range(PASSES):
-                quantise_rows(w2_raw[a, piece], ACT.Copy, w2_w[a], w2_s[a], piece)
+                interleave(grouped[:, a, :, :], w2_raw[a, piece], ACT.Copy)
+            nc.vector.quantize_mx(
+                w2_w[piece][:].rearrange("p a w -> p (a w)").bitcast(FP8X4),
+                w2_s[piece][:].rearrange("p a w -> p (a w)"),
+                grouped[:].rearrange("p a w t -> p (a w t)"),
+            )
 
         def entries(idx, first, count):
             return idx[:, first // PER_COL : (first + count) // PER_COL]
@@ -155,13 +163,18 @@ def tile_list_fibre_nonlinear_deinterleave_kernel(
         def gather_words(a, first, count):
             nc.vector.tensor_copy(v_w[a][:, first : first + count], tab_w[a][:].bitcast(U32).indirect(entries(idx1, first, count)))
 
+        h_done = []
+
         def scatter_h(c, first, count):
-            acc = psum.tile([P, BANK], F32, name="acc", tag="acc", bufs=4)
+            acc = bank_tile(len(h_done) % (4 if c < ROW_TILES - 1 else 2))
+            h_done.append((c, first))
             rows = slice(c * P, (c + 1) * P)
+            piece, w2_first = divmod(c * P, PIECE)
+            w2_cols = slice(w2_first, w2_first + P)
             cols = slice(first, first + count)
             for a in range(PASSES):
                 nc.tensor.matmul_mx(
-                    acc[:, :count], w2_w[a][:, rows].bitcast(FP8X4), w2_s[a][:, rows],
+                    acc[:, :count], w2_w[piece][:, a, w2_cols].bitcast(FP8X4), w2_s[piece][:, a, w2_cols],
                     sq_w[a][:, cols].bitcast(FP8X4), sq_s[a][:, cols], start=(a == 0), stop=False,
                 )
             width = BANK if count == BANK else P
@@ -183,39 +196,44 @@ def tile_list_fibre_nonlinear_deinterleave_kernel(
             nc.scalar.activation(gd[:], d[c][:], ACT.Identity, bias=gain_col[:, c : c + 1], scale=1.0)
             return gd
 
-        def z_rows(c, gd, zt, first, count, step):
-            y = ring.tile([P, M], F32, name="y", bufs=2, align_bytes=64)
+        def z_rows(c, gd, zt, first, count, banks):
+            y = ring.tile([P, M], F32, name="y", bufs=3, align_bytes=64)
             nc.vector.tensor_tensor(
                 y[:, :count], pages[c % 2][:].indirect(entries(idx3, first, count)), gd[:, first : first + count], MULT
             )
-            for lo in range(0, count, step):
-                blocks = step // P
-                bank = psum.tile([P, BANK], F32, name="zt_bank", bufs=2)
+            step = count // len(banks)
+            blocks = step // P
+            quarter = slice(32 * (c % PACK), 32 * (c % PACK + 1))
+            for number, lo in zip(banks, range(0, count, step)):
+                bank = bank_tile(number)
                 for src, off, is_last in ((d[c], first + lo, False), (y, lo, True)):
                     for k in range(blocks):
                         nc.tensor.matmul(
                             bank[:, k * P : (k + 1) * P], src[:, off + k * P : off + (k + 1) * P], ident[:],
                             is_transpose=True, start=(k == 0 and not is_last), stop=(is_last and k == blocks - 1),
                         )
-                quarter = c % PACK
-                for part in range(0, step, PIECE):
-                    nc.scalar.copy(
-                        zt[(first + lo + part) // PIECE][:, :, :, 32 * quarter : 32 * (quarter + 1), :],
-                        bank[:, part : part + PIECE].rearrange("m (k p u e) -> m k u p e", k=2, u=2, e=2),
-                    )
+                for (start, width), tile in zt.items():
+                    part = start - (first + lo)
+                    if 0 <= part < step:
+                        nc.scalar.copy(
+                            tile[:, :, :, quarter, :],
+                            bank[:, part : part + width].rearrange("m (k p u e) -> m k u p e", p=32, u=2, e=2),
+                        )
 
-        def quantise_z(a, zt, first, count):
+        def quantise_z(a, tile, first, count, banks):
             words = ring.tile([P, BANK, 2], F32, name="z_words", bufs=2, align_bytes=64)
-            for lo in range(0, count, PIECE):
-                bank = psum.tile([P, 2, 2, P], F32, name="zb_bank", bufs=2)
-                for k in range(2):
+            step = count // len(banks)
+            blocks = step // P
+            for number, lo in zip(banks, range(0, count, step)):
+                bank = bank_tile(number)
+                turned = bank[:, : 2 * step].rearrange("p (k u m) -> p k u m", u=2, m=P)
+                for k in range(blocks):
                     for u in range(2):
                         nc.tensor.transpose(
-                            bank[:, k, u, :], zt[(first + lo) // PIECE][:, k, u, :, :].rearrange("m p e -> m (p e)").bitcast(F32), ident[:]
+                            turned[:, k, u, :], tile[:, lo // P + k, u, :, :].rearrange("m p e -> m (p e)").bitcast(F32), ident[:]
                         )
                 nc.scalar.copy(
-                    words[:, lo : lo + PIECE, :].rearrange("p (k m) u -> p k m u", k=2),
-                    bank[:].rearrange("p k u m -> p k m u"),
+                    words[:, lo : lo + step, :].rearrange("p (k m) u -> p k m u", m=P), turned.rearrange("p k u m -> p k m u")
                 )
             cols = slice(first, first + count)
             nc.vector.quantize_mx(
@@ -223,26 +241,35 @@ def tile_list_fibre_nonlinear_deinterleave_kernel(
                 words[:, :count, :].rearrange("p m u -> p (m u)").bitcast(BF16),
             )
 
-        def out_piece(first):
-            cols = slice(first, first + PIECE)
-            staged = ring.tile([P, N // P, PIECE], F32, name="staged", bufs=3, align_bytes=64)
-            for half in range(2):
-                acc = psum.tile([P, BANK], F32, name="acc", tag="acc", bufs=4)
-                for a in range(PASSES):
-                    for k in range(2):
-                        n0 = (2 * half + k) * P
-                        nc.tensor.matmul_mx(
-                            acc[:, k * PIECE : (k + 1) * PIECE],
-                            w3_w[:, a, n0 : n0 + P].bitcast(FP8X4), w3_s[:, a, n0 : n0 + P],
-                            z_w[a][:, cols].bitcast(FP8X4), z_s[a][:, cols],
-                            start=(a == 0 and k == 0), stop=(a == PASSES - 1 and k == 1),
-                        )
-                dst = staged[:, 2 * half : 2 * half + 2, :].rearrange("p k m -> p (k m)")
-                if half == 0:
-                    nc.scalar.copy(dst, acc[:])
-                else:
-                    nc.vector.tensor_copy(dst, acc[:])
-            nc.sync.dma_start(out[:, cols].rearrange("(k p) m -> p k m", p=P), staged[:])
+        def open_out(first, count, banks):
+            per_bank = N // P // len(banks)
+            accs = [bank_tile(number) for number in banks]
+            for a in range(PASSES - 1):
+                out_pass(a, first, count, accs, per_bank)
+            return accs
+
+        def out_pass(a, first, count, accs, per_bank):
+            cols = slice(first, first + count)
+            for half, acc in enumerate(accs):
+                for k in range(per_bank):
+                    n0 = (per_bank * half + k) * P
+                    nc.tensor.matmul_mx(
+                        acc[:, k * count : (k + 1) * count],
+                        w3_w[:, a, n0 : n0 + P].bitcast(FP8X4), w3_s[:, a, n0 : n0 + P],
+                        z_w[a][:, cols].bitcast(FP8X4), z_s[a][:, cols],
+                        start=(a == 0 and k == 0), stop=(a == PASSES - 1 and k == per_bank - 1),
+                    )
+
+        def close_out(first, count, accs, engines):
+            per_bank = N // P // len(accs)
+            out_pass(PASSES - 1, first, count, accs, per_bank)
+            out_rows = out[:, first : first + count].rearrange("(k p) m -> p k m", p=P)
+            for half, (acc, copy) in enumerate(zip(accs, engines)):
+                staged = ring.tile([P, BANK], F32, name="staged", bufs=6, align_bytes=64)
+                copy(staged[:], acc[:])
+                nc.sync.dma_start(
+                    out_rows[:, per_bank * half : per_bank * (half + 1), :], staged[:].rearrange("p (k m) -> p k m", k=per_bank)
+                )
 
         gather_words(0, 0, S)
         for a in range(PASSES):
@@ -259,15 +286,17 @@ def tile_list_fibre_nonlinear_deinterleave_kernel(
                     gather_words(1, PIECE, S - PIECE)
         quantise_w2(1)
 
-        gain_bank = psum.tile([P, 2, 2, P], F32, name="zb_bank", bufs=2)
-        nc.tensor.transpose(gain_bank[:, 0, 0, :], gain_rows[:], ident[:])
-        nc.scalar.copy(gain_col[:], gain_bank[:, 0, 0, :ROW_TILES])
+        gain_bank = bank_tile(6)
+        nc.tensor.transpose(gain_bank[:, :P], gain_rows[:], ident[:])
+        nc.scalar.copy(gain_col[:], gain_bank[:, :ROW_TILES])
 
-        def new_zt():
-            return [ring.tile([P, 2, 2, P, 2], BF16, name="zt", bufs=M // PIECE, align_bytes=64) for piece in range(M // PIECE)]
+        def new_zt(a, parts):
+            return {
+                (first, count): held([P, count // P, 2, P, 2], BF16, f"zt{a}_{first}") for first, count in parts
+            }
 
-        zt = new_zt()
-        z_rows(0, gain_plus_disp(0), zt, 0, M, BANK)
+        zt = new_zt(0, [(0, BANK), (BANK, BANK)])
+        z_rows(0, gain_plus_disp(0), zt, 0, M, (4, 5))
         for c in range(1, ROW_TILES - 1):
             if c in (2, 4):
                 quantise_w2(c // 2 + 1)
@@ -275,16 +304,22 @@ def tile_list_fibre_nonlinear_deinterleave_kernel(
                 scatter_h(c, BANK, BANK)
             scatter_h(c + 1, 0, BANK)
             if c == PACK:
-                zt = new_zt()
-            z_rows(c, gain_plus_disp(c), zt, 0, M, BANK)
+                zt = new_zt(1, TAIL_PARTS)
+            z_rows(c, gain_plus_disp(c), zt, 0, M, (4, 5) if c < ROW_TILES - 2 else (2, 3, 4, 5))
             if c == PACK - 1:
-                for first in range(0, M, BANK):
-                    quantise_z(0, zt, first, BANK)
+                for (first, count), tile in zt.items():
+                    quantise_z(0, tile, first, count, (6, 7))
         last = ROW_TILES - 1
         scatter_h(last, BANK, BANK)
         gd = gain_plus_disp(last)
+        out_banks = ((2, 3), (4, 5), (0, 1), (2,), (3,))
+        both = (nc.scalar.copy, nc.vector.tensor_copy)
+        out_engines = (both, both, both, both[:1], both[1:])
+        accs = {i: open_out(*TAIL_PARTS[i], out_banks[i]) for i in range(2)}
         for first in range(0, M, PIECE):
-            z_rows(last, gd, zt, first, PIECE, PIECE)
-        for first in range(0, M, PIECE):
-            quantise_z(1, zt, first, PIECE)
-            out_piece(first)
+            z_rows(last, gd, zt, first, PIECE, (first // PIECE % 2,))
+        for i, (first, count) in enumerate(TAIL_PARTS):
+            quantise_z(1, zt[first, count], first, count, (6 + i % 2,))
+            if i not in accs:
+                accs[i] = open_out(first, count, out_banks[i])
+            close_out(first, count, accs[i], out_engines[i])

@@ -16,6 +16,7 @@ FP8X4 = mybir.dt.float8_e4m3fn_x4
 FP4X4 = mybir.dt.float4_e2m1fn_x4
 ACT = mybir.ActivationFunctionType
 MULT = mybir.AluOpType.mult
+ADD = mybir.AluOpType.add
 
 P = 128
 PACK = 4
@@ -25,7 +26,9 @@ BANK = 512
 PIECE = 256
 ROW_TILES = H // P
 PER_COL = 16
-TAIL_PARTS = [(0, 256), (256, 256), (512, 256), (768, 128), (896, 128)]
+RAW_BUFS = 8
+PAGES = 3
+TAIL_PARTS = [(first, PIECE) for first in range(0, M, PIECE)]
 
 
 def tile_list_fibre_nonlinear_deinterleave_kernel(
@@ -62,19 +65,18 @@ def tile_list_fibre_nonlinear_deinterleave_kernel(
         z_w = [held([P, M], U32, f"z_w{a}") for a in range(PASSES)]
         z_s = [held([P, M], U8, f"z_s{a}") for a in range(PASSES)]
         weights = held([P, S], F32, "weights")
-        pages = [held([P, T2], F32, f"page{i}") for i in range(2)]
+        pages = [held([P, T2], F32, f"page{i}") for i in range(PAGES - 1)]
         ident = held([P, P], F32, "ident")
         gain_rows = held([P, P], F32, "gain_rows")
         gain_col = held([P, ROW_TILES], F32, "gain_col")
-        warm = held([P, 2], F32, "warm")
+        h = {c: held([P, S], F32, f"h{c}") for c in range(PAGES)}
+        d = [held([P, M], F32, f"d{c}") for c in range(ROW_TILES)]
 
         nc.vector.memset(tab_s[:].rearrange("p a t -> p (a t)").bitcast(I32), 0)
         nc.vector.memset(w1_s[:].rearrange("p a t -> p (a t)").bitcast(I32), 0)
-        nc.vector.memset(pages[0][:], 0.0)
-        nc.gpsimd.memset(warm[:], 0.0)
-        nc.gpsimd.memset(pages[1][:], 0.0)
+        for page in pages:
+            nc.vector.memset(page[:], 0.0)
         nc.gpsimd.memset(w3_s[:].rearrange("p a t -> p (a t)").bitcast(I32), 0)
-        nc.scalar.activation(warm[:, 1:2], warm[:, 0:1], ACT.Tanh)
         make_identity(nc, ident[:])
         nc.gpsimd.memset(gain_rows[:], 0.0)
 
@@ -89,18 +91,21 @@ def tile_list_fibre_nonlinear_deinterleave_kernel(
             nc.sync.dma_start(tab_w[a][:], tab_words[a].rearrange("p t i -> p (t i)").bitcast(I32))
 
         def load_rows(matrix, a, piece):
-            raw = ring.tile([P, PACK, PIECE], F32, name="raw", tag="raw", bufs=14, align_bytes=64)
+            if matrix is xn and a == PASSES - 1 and piece > 0:
+                raw = held([P, PACK, PIECE], F32, f"xn_last{piece}")
+            elif a == PASSES - 1 and piece == 1:
+                raw = held([P, PACK, PIECE], F32, "w2_last")
+            else:
+                raw = ring.tile([P, PACK, PIECE], F32, name="raw", tag="raw", bufs=RAW_BUFS, align_bytes=64)
             rows = matrix[a * K_PASS : (a + 1) * K_PASS, piece * PIECE : (piece + 1) * PIECE]
             nc.sync.dma_start(raw[:], rows.rearrange("(p t) w -> p t w", t=PACK))
             return raw
 
         def load_disp(c):
-            raw = ring.tile([P, M], F32, name="raw", tag="raw", bufs=14, align_bytes=64)
-            nc.sync.dma_start(raw[:], disp[c * P : (c + 1) * P, :])
-            return raw
+            nc.sync.dma_start(d[c][:], disp[c * P : (c + 1) * P, :])
 
         w1_bytes = w1_words.rearrange("a p n -> p a n")
-        xn_raw, w2_raw, d = {}, {}, {}
+        xn_raw, w2_raw = {}, {}
         nc.sync.dma_start(idx1[:], offs)
         nc.sync.dma_start(idx2[:], offs2)
         nc.sync.dma_start(idx3[:], offs3)
@@ -117,21 +122,16 @@ def tile_list_fibre_nonlinear_deinterleave_kernel(
         for a in range(PASSES):
             xn_raw[a, 1] = load_rows(xn, a, 1)
         nc.sync.dma_start(weights[:, PIECE:], wgs[:, PIECE:])
-        for piece in (2, 3):
-            for a in range(PASSES):
-                xn_raw[a, piece] = load_rows(xn, a, piece)
         nc.sync.dma_start(w1_rest[:].bitcast(I32), w1_bytes[:, :, 2 * PIECE :].bitcast(I32))
-        for a in range(PASSES):
-            w2_raw[a, 1] = load_rows(w2, a, 1)
+        for matrix, raws, piece in ((w2, w2_raw, 1), (xn, xn_raw, 2), (xn, xn_raw, 3)):
+            for a in range(PASSES):
+                raws[a, piece] = load_rows(matrix, a, piece)
         nc.sync.dma_start(gain_rows[:ROW_TILES, :], gain.rearrange("(c p) -> c p", p=P))
-        for piece in range(1, 4):
-            for c in (2 * piece - 2, 2 * piece - 1):
-                d[c] = load_disp(c)
-            if piece < 3:
-                for a in range(PASSES):
-                    w2_raw[a, piece + 1] = load_rows(w2, a, piece + 1)
-        for c in (6, 7):
-            d[c] = load_disp(c)
+        for piece, tiles in ((2, range(0, 3)), (3, range(3, ROW_TILES))):
+            for a in range(PASSES):
+                w2_raw[a, piece] = load_rows(w2, a, piece)
+            for c in tiles:
+                load_disp(c)
         nc.sync.dma_start(w3_w[:], w3_words.rearrange("a p n i -> p a (n i)").bitcast(I32))
         load_scale_rows(nc.sync, w3_s, w3_scales)
 
@@ -148,7 +148,7 @@ def tile_list_fibre_nonlinear_deinterleave_kernel(
                 nc.vector.quantize_mx(sq_w[a][:, cols].bitcast(FP8X4), sq_s[a][:, cols], grouped[:].rearrange("p w t -> p (w t)"))
 
         def quantise_w2(piece):
-            grouped = ring.tile([P, PASSES, PIECE, PACK], BF16, name="w2_grouped", bufs=1, align_bytes=64)
+            grouped = ring.tile([P, PASSES, PIECE, PACK], BF16, name="w2_grouped", bufs=2, align_bytes=64)
             for a in range(PASSES):
                 interleave(grouped[:, a, :, :], w2_raw[a, piece], ACT.Copy)
             nc.vector.quantize_mx(
@@ -163,11 +163,8 @@ def tile_list_fibre_nonlinear_deinterleave_kernel(
         def gather_words(a, first, count):
             nc.vector.tensor_copy(v_w[a][:, first : first + count], tab_w[a][:].bitcast(U32).indirect(entries(idx1, first, count)))
 
-        h_done = []
-
-        def scatter_h(c, first, count):
-            acc = bank_tile(len(h_done) % (4 if c < ROW_TILES - 1 else 2))
-            h_done.append((c, first))
+        def make_h(c, first, count, number, values):
+            acc = bank_tile(number)
             rows = slice(c * P, (c + 1) * P)
             piece, w2_first = divmod(c * P, PIECE)
             w2_cols = slice(w2_first, w2_first + P)
@@ -187,41 +184,43 @@ def tile_list_fibre_nonlinear_deinterleave_kernel(
                         v_w[a][:, part].bitcast(FP8X4), v_s[a][:, part],
                         start=False, stop=(a == PASSES - 1 and lo + width == count),
                     )
-            h = ring.tile([P, BANK], F32, name="h", bufs=6, align_bytes=64)
-            nc.scalar.activation(h[:, :count], acc[:, :count], ACT.Tanh)
-            nc.vector.tensor_tensor(pages[c % 2][:].indirect(entries(idx2, first, count)), h[:, :count], weights[:, cols], MULT)
+            nc.scalar.activation(values, acc[:, :count], ACT.Tanh)
+
+        def scatter_h(c, first, count, values):
+            cols = slice(first, first + count)
+            nc.vector.tensor_tensor(pages[c % PAGES][:].indirect(entries(idx2, first, count)), values, weights[:, cols], MULT)
 
         def gain_plus_disp(c):
-            gd = ring.tile([P, M], F32, name="gd", bufs=2, align_bytes=64)
+            gd = held([P, M], F32, {0: "gd0", 1: "gd1", 6: "sq_w0", 7: "gd7"}.get(c, f"h{(c - 1) % 4}"))
             nc.scalar.activation(gd[:], d[c][:], ACT.Identity, bias=gain_col[:, c : c + 1], scale=1.0)
             return gd
 
-        def z_rows(c, gd, zt, first, count, banks):
-            y = ring.tile([P, M], F32, name="y", bufs=3, align_bytes=64)
-            nc.vector.tensor_tensor(
-                y[:, :count], pages[c % 2][:].indirect(entries(idx3, first, count)), gd[:, first : first + count], MULT
-            )
+        def z_rows(tiles, gd, zt, first, count, banks):
+            for c in tiles:
+                nc.vector.tensor_tensor(
+                    h[c][:, first : first + count], pages[c % PAGES][:].indirect(entries(idx3, first, count)),
+                    gd[c][:, first : first + count], MULT,
+                )
             step = count // len(banks)
-            blocks = step // P
-            quarter = slice(32 * (c % PACK), 32 * (c % PACK + 1))
-            for number, lo in zip(banks, range(0, count, step)):
+            rows = P * len(tiles)
+            quarters = slice(32 * (tiles[0] % PACK), 32 * (tiles[-1] % PACK + 1))
+            for number, lo in zip(banks, range(first, first + count, step)):
                 bank = bank_tile(number)
-                for src, off, is_last in ((d[c], first + lo, False), (y, lo, True)):
-                    for k in range(blocks):
-                        nc.tensor.matmul(
-                            bank[:, k * P : (k + 1) * P], src[:, off + k * P : off + (k + 1) * P], ident[:],
-                            is_transpose=True, start=(k == 0 and not is_last), stop=(is_last and k == blocks - 1),
-                        )
+                turns = [(src, i, c, k) for src in (d, h) for i, c in enumerate(tiles) for k in range(step // P)]
+                for n, (src, i, c, k) in enumerate(turns):
+                    nc.tensor.matmul(
+                        bank[:, k * rows + i * P : k * rows + (i + 1) * P], src[c][:, lo + k * P : lo + (k + 1) * P], ident[:],
+                        is_transpose=True, start=(n == 0), stop=(n == len(turns) - 1),
+                    )
                 for (start, width), tile in zt.items():
-                    part = start - (first + lo)
-                    if 0 <= part < step:
+                    if lo <= start < lo + step:
+                        part = bank[:, (start - lo) // P * rows : (start - lo + width) // P * rows]
                         nc.scalar.copy(
-                            tile[:, :, :, quarter, :],
-                            bank[:, part : part + width].rearrange("m (k p u e) -> m k u p e", p=32, u=2, e=2),
+                            tile[:, :, :, quarters, :], part.rearrange("m (k p u e) -> m k u p e", p=rows // PACK, u=2, e=2)
                         )
 
-        def quantise_z(a, tile, first, count, banks):
-            words = ring.tile([P, BANK, 2], F32, name="z_words", bufs=2, align_bytes=64)
+        def quantise_z(a, tile, first, count, banks, copy):
+            words = ring.tile([P, BANK, 2], F32, name="z_words", tag="raw", bufs=RAW_BUFS, align_bytes=64)
             step = count // len(banks)
             blocks = step // P
             for number, lo in zip(banks, range(0, count, step)):
@@ -232,7 +231,7 @@ def tile_list_fibre_nonlinear_deinterleave_kernel(
                         nc.tensor.transpose(
                             turned[:, k, u, :], tile[:, lo // P + k, u, :, :].rearrange("m p e -> m (p e)").bitcast(F32), ident[:]
                         )
-                nc.scalar.copy(
+                copy(
                     words[:, lo : lo + step, :].rearrange("p (k m) u -> p k m u", m=P), turned.rearrange("p k u m -> p k m u")
                 )
             cols = slice(first, first + count)
@@ -241,35 +240,20 @@ def tile_list_fibre_nonlinear_deinterleave_kernel(
                 words[:, :count, :].rearrange("p m u -> p (m u)").bitcast(BF16),
             )
 
-        def open_out(first, count, banks):
-            per_bank = N // P // len(banks)
-            accs = [bank_tile(number) for number in banks]
-            for a in range(PASSES - 1):
-                out_pass(a, first, count, accs, per_bank)
-            return accs
-
-        def out_pass(a, first, count, accs, per_bank):
-            cols = slice(first, first + count)
-            for half, acc in enumerate(accs):
-                for k in range(per_bank):
-                    n0 = (per_bank * half + k) * P
-                    nc.tensor.matmul_mx(
-                        acc[:, k * count : (k + 1) * count],
-                        w3_w[:, a, n0 : n0 + P].bitcast(FP8X4), w3_s[:, a, n0 : n0 + P],
-                        z_w[a][:, cols].bitcast(FP8X4), z_s[a][:, cols],
-                        start=(a == 0 and k == 0), stop=(a == PASSES - 1 and k == per_bank - 1),
-                    )
-
-        def close_out(first, count, accs, engines):
-            per_bank = N // P // len(accs)
-            out_pass(PASSES - 1, first, count, accs, per_bank)
-            out_rows = out[:, first : first + count].rearrange("(k p) m -> p k m", p=P)
-            for half, (acc, copy) in enumerate(zip(accs, engines)):
-                staged = ring.tile([P, BANK], F32, name="staged", bufs=6, align_bytes=64)
-                copy(staged[:], acc[:])
-                nc.sync.dma_start(
-                    out_rows[:, per_bank * half : per_bank * (half + 1), :], staged[:].rearrange("p (k m) -> p k m", k=per_bank)
+        def out_pass(a, first, half, acc, start, stop):
+            cols = slice(first, first + PIECE)
+            for k in range(2):
+                n0 = (2 * half + k) * P
+                nc.tensor.matmul_mx(
+                    acc[:, k * PIECE : (k + 1) * PIECE],
+                    w3_w[:, a, n0 : n0 + P].bitcast(FP8X4), w3_s[:, a, n0 : n0 + P],
+                    z_w[a][:, cols].bitcast(FP8X4), z_s[a][:, cols],
+                    start=(start and k == 0), stop=(stop and k == 1),
                 )
+
+        def store_out(first, half, values):
+            out_rows = out[:, first : first + PIECE].rearrange("(k p) m -> p k m", p=P)
+            nc.sync.dma_start(out_rows[:, 2 * half : 2 * half + 2, :], values.rearrange("p (k m) -> p k m", k=2))
 
         gather_words(0, 0, S)
         for a in range(PASSES):
@@ -277,14 +261,37 @@ def tile_list_fibre_nonlinear_deinterleave_kernel(
         quantise_sq(0)
         quantise_w2(0)
         gather_words(1, 0, PIECE)
-        for piece in range(4):
-            if piece > 0:
-                quantise_sq(piece)
-            for c in range(2):
-                scatter_h(c, piece * PIECE, PIECE)
-                if piece == 0 and c == 0:
-                    gather_words(1, PIECE, S - PIECE)
+        def head_piece(c, piece, values):
+            make_h(c, piece * PIECE, PIECE, (PAGES * piece + c) % 4, values)
+            scatter_h(c, piece * PIECE, PIECE, values)
+
+        def piece_of(c, piece):
+            return h[c][:, piece * PIECE : (piece + 1) * PIECE]
+
+        def spent(name):
+            return held([P, PIECE], F32, name)[:]
+
+        head_piece(0, 0, piece_of(0, 0))
+        gather_words(1, PIECE, S - PIECE)
+        pages.append(held([P, T2], F32, "tab_w1"))
+        nc.gpsimd.memset(pages[-1][:], 0.0)
+        quantise_sq(1)
+        head_piece(1, 0, spent("xn_last1"))
+        head_piece(0, 1, piece_of(0, 1))
         quantise_w2(1)
+        head_piece(1, 1, spent("w2_last"))
+        head_piece(2, 0, piece_of(2, 0))
+        for piece in (2, 3):
+            quantise_sq(piece)
+            head_piece(2, piece - 1, spent(f"xn_last{piece}"))
+            for c in range(2):
+                head_piece(c, piece, piece_of(c, piece))
+        head_piece(2, 3, piece_of(2, 3))
+
+        def make_h_tile(c, banks):
+            h[c] = held([P, S], F32, f"h{c % 4}")
+            for half in range(2):
+                make_h(c, half * BANK, BANK, banks[half], h[c][:, half * BANK : (half + 1) * BANK])
 
         gain_bank = bank_tile(6)
         nc.tensor.transpose(gain_bank[:, :P], gain_rows[:], ident[:])
@@ -295,31 +302,52 @@ def tile_list_fibre_nonlinear_deinterleave_kernel(
                 (first, count): held([P, count // P, 2, P, 2], BF16, f"zt{a}_{first}") for first, count in parts
             }
 
+        last = ROW_TILES - 1
+        gd = {c: gain_plus_disp(c) for c in (0, 1, last)}
+        quantise_w2(2)
+        make_h_tile(3, (0, 1))
+        quantise_w2(3)
         zt = new_zt(0, [(0, BANK), (BANK, BANK)])
-        z_rows(0, gain_plus_disp(0), zt, 0, M, (4, 5))
-        for c in range(1, ROW_TILES - 1):
-            if c in (2, 4):
-                quantise_w2(c // 2 + 1)
-            if c > 1:
-                scatter_h(c, BANK, BANK)
-            scatter_h(c + 1, 0, BANK)
+        for c in range(last - 1):
+            pair = (2 * (c % 2), 2 * (c % 2) + 1)
             if c == PACK:
                 zt = new_zt(1, TAIL_PARTS)
-            z_rows(c, gain_plus_disp(c), zt, 0, M, (4, 5) if c < ROW_TILES - 2 else (2, 3, 4, 5))
+            z_rows([c], gd, zt, 0, M, pair)
+            if c > 0:
+                scatter_h(c + 2, 0, S, h[c + 2][:])
+                gd[c + 1] = gain_plus_disp(c + 1)
+            if 0 < c <= last - 3:
+                make_h_tile(c + 3, pair)
             if c == PACK - 1:
                 for (first, count), tile in zt.items():
-                    quantise_z(0, tile, first, count, (6, 7))
-        last = ROW_TILES - 1
-        scatter_h(last, BANK, BANK)
-        gd = gain_plus_disp(last)
-        out_banks = ((2, 3), (4, 5), (0, 1), (2,), (3,))
-        both = (nc.scalar.copy, nc.vector.tensor_copy)
-        out_engines = (both, both, both, both[:1], both[1:])
-        accs = {i: open_out(*TAIL_PARTS[i], out_banks[i]) for i in range(2)}
-        for first in range(0, M, PIECE):
-            z_rows(last, gd, zt, first, PIECE, (first // PIECE % 2,))
-        for i, (first, count) in enumerate(TAIL_PARTS):
-            quantise_z(1, zt[first, count], first, count, (6 + i % 2,))
-            if i not in accs:
-                accs[i] = open_out(first, count, out_banks[i])
-            close_out(first, count, accs[i], out_engines[i])
+                    quantise_z(0, tile, first, count, (4, 5), nc.scalar.copy)
+        early, accs = {}, {}
+        for i in range(2):
+            early[i] = held([P, 2, BANK], F32, f"xn_last{i + 1}")
+            for half in range(2):
+                acc = bank_tile(4 + 2 * i + half)
+                out_pass(0, i * PIECE, half, acc, True, True)
+                nc.scalar.copy(early[i][:, half, :], acc[:])
+        for i in range(2, 4):
+            for half in range(2):
+                accs[i, half] = bank_tile(2 * i + half)
+                out_pass(0, i * PIECE, half, accs[i, half], True, False)
+        for i in range(5):
+            if i < 4:
+                z_rows([last - 1, last], gd, zt, i * PIECE, PIECE, (i,))
+            if i > 0:
+                first = (i - 1) * PIECE
+                quantise_z(1, zt[first, PIECE], first, PIECE, (i - 1,), nc.vector.tensor_copy if i == 2 else nc.scalar.copy)
+        for i in range(2):
+            for half in range(2):
+                acc = bank_tile(2 * i + half)
+                out_pass(1, i * PIECE, half, acc, True, True)
+                nc.vector.tensor_tensor(early[i][:, half, :], acc[:], early[i][:, half, :], ADD)
+                store_out(i * PIECE, half, early[i][:, half, :])
+        for i in range(2, 4):
+            for half in range(2):
+                out_pass(1, i * PIECE, half, accs[i, half], False, True)
+                staged = ring.tile([P, BANK], F32, name="staged", tag="raw", bufs=RAW_BUFS, align_bytes=64)
+                copy = nc.vector.tensor_copy if (i, half) == (3, 1) else nc.scalar.copy
+                copy(staged[:], accs[i, half][:])
+                store_out(i * PIECE, half, staged[:])

@@ -62,29 +62,27 @@ def tile_list_fibre_nonlinear_deinterleave_kernel(
         sq_s = [held([P, S], U8, f"sq_s{a}") for a in range(PASSES)]
         w2_w = [held([P, PASSES, PIECE], U32, f"w2_w{piece}") for piece in range(H // PIECE)]
         w2_s = [held([P, PASSES, PIECE], U8, f"w2_s{piece}") for piece in range(H // PIECE)]
-        z_w = [held([P, M], U32, f"z_w{a}") for a in range(PASSES)]
+        z_w = {}
         z_s = [held([P, M], U8, f"z_s{a}") for a in range(PASSES)]
         weights = held([P, S], F32, "weights")
-        pages = [held([P, T2], F32, f"page{i}") for i in range(PAGES - 1)]
-        ident = held([P, P], F32, "ident")
+        pages = [held([P, T2], F32, f"page{i}") for i in range(PAGES)]
         gain_rows = held([P, P], F32, "gain_rows")
         gain_col = held([P, ROW_TILES], F32, "gain_col")
         h = {c: held([P, S], F32, f"h{c}") for c in range(PAGES)}
         d = [held([P, M], F32, f"d{c}") for c in range(ROW_TILES)]
 
-        nc.vector.memset(tab_s[:].rearrange("p a t -> p (a t)").bitcast(I32), 0)
+        nc.gpsimd.memset(tab_s[:].rearrange("p a t -> p (a t)").bitcast(I32), 0)
         nc.vector.memset(w1_s[:].rearrange("p a t -> p (a t)").bitcast(I32), 0)
         for page in pages:
             nc.vector.memset(page[:], 0.0)
-        nc.gpsimd.memset(w3_s[:].rearrange("p a t -> p (a t)").bitcast(I32), 0)
-        make_identity(nc, ident[:])
-        nc.gpsimd.memset(gain_rows[:], 0.0)
+        nc.vector.memset(w3_s[:].rearrange("p a t -> p (a t)").bitcast(I32), 0)
+        nc.vector.memset(gain_rows[:], 0.0)
 
         def load_scale_rows(queue, plane, scales):
-            for q in range(4):
+            for r in range(4):
                 queue.dma_start(
-                    plane[32 * q : 32 * q + 4, :, :].bitcast(I32),
-                    scales[:, 4 * q : 4 * q + 4, :].rearrange("a r n -> r a n").bitcast(I32),
+                    plane[r:P:32, :, :].bitcast(I32),
+                    scales[:, r:16:4, :].rearrange("a q n -> q a n").bitcast(I32),
                 )
 
         def load_table_words(a):
@@ -106,32 +104,36 @@ def tile_list_fibre_nonlinear_deinterleave_kernel(
 
         w1_bytes = w1_words.rearrange("a p n -> p a n")
         xn_raw, w2_raw = {}, {}
+        load_scale_rows(nc.sync, tab_s, tab_scales)
         nc.sync.dma_start(idx1[:], offs)
         nc.sync.dma_start(idx2[:], offs2)
         nc.sync.dma_start(idx3[:], offs3)
-        nc.sync.dma_start(weights[:, :PIECE], wgs[:, :PIECE])
-        load_table_words(0)
-        load_scale_rows(nc.scalar, tab_s, tab_scales)
+        nc.sync.dma_start(w1_head[:].bitcast(I32), w1_bytes[:, :, : 2 * PIECE].bitcast(I32))
         for a in range(PASSES):
             xn_raw[a, 0] = load_rows(xn, a, 0)
         for a in range(PASSES):
             w2_raw[a, 0] = load_rows(w2, a, 0)
-        load_table_words(1)
+        load_table_words(0)
         load_scale_rows(nc.sync, w1_s, w1_scales)
-        nc.sync.dma_start(w1_head[:].bitcast(I32), w1_bytes[:, :, : 2 * PIECE].bitcast(I32))
+        load_table_words(1)
+        nc.sync.dma_start(weights[:, :PIECE], wgs[:, :PIECE])
         for a in range(PASSES):
             xn_raw[a, 1] = load_rows(xn, a, 1)
         nc.sync.dma_start(weights[:, PIECE:], wgs[:, PIECE:])
+        for a in range(PASSES):
+            w2_raw[a, 1] = load_rows(w2, a, 1)
         nc.sync.dma_start(w1_rest[:].bitcast(I32), w1_bytes[:, :, 2 * PIECE :].bitcast(I32))
-        for matrix, raws, piece in ((w2, w2_raw, 1), (xn, xn_raw, 2), (xn, xn_raw, 3)):
+        for piece in (2, 3):
             for a in range(PASSES):
-                raws[a, piece] = load_rows(matrix, a, piece)
+                xn_raw[a, piece] = load_rows(xn, a, piece)
         nc.sync.dma_start(gain_rows[:ROW_TILES, :], gain.rearrange("(c p) -> c p", p=P))
-        for piece, tiles in ((2, range(0, 3)), (3, range(3, ROW_TILES))):
-            for a in range(PASSES):
-                w2_raw[a, piece] = load_rows(w2, a, piece)
+        for tiles, piece in ((range(0, 2), 2), (range(2, 3), 3)):
             for c in tiles:
                 load_disp(c)
+            for a in range(PASSES):
+                w2_raw[a, piece] = load_rows(w2, a, piece)
+        for c in range(3, ROW_TILES):
+            load_disp(c)
         nc.sync.dma_start(w3_w[:], w3_words.rearrange("a p n i -> p a (n i)").bitcast(I32))
         load_scale_rows(nc.sync, w3_s, w3_scales)
 
@@ -148,7 +150,7 @@ def tile_list_fibre_nonlinear_deinterleave_kernel(
                 nc.vector.quantize_mx(sq_w[a][:, cols].bitcast(FP8X4), sq_s[a][:, cols], grouped[:].rearrange("p w t -> p (w t)"))
 
         def quantise_w2(piece):
-            grouped = ring.tile([P, PASSES, PIECE, PACK], BF16, name="w2_grouped", bufs=2, align_bytes=64)
+            grouped = held([P, PASSES, PIECE, PACK], BF16, ("w2_grouped0", "w2_grouped1", "xn_last3", "tab_w0")[piece])
             for a in range(PASSES):
                 interleave(grouped[:, a, :, :], w2_raw[a, piece], ACT.Copy)
             nc.vector.quantize_mx(
@@ -191,35 +193,41 @@ def tile_list_fibre_nonlinear_deinterleave_kernel(
             nc.vector.tensor_tensor(pages[c % PAGES][:].indirect(entries(idx2, first, count)), values, weights[:, cols], MULT)
 
         def gain_plus_disp(c):
-            gd = held([P, M], F32, {0: "gd0", 1: "gd1", 6: "sq_w0", 7: "gd7"}.get(c, f"h{(c - 1) % 4}"))
+            gd = held([P, M], F32, {0: "tab_w0", 1: "tab_w1", 6: "gd6", 7: "gd7"}.get(c, f"h{(c - 1) % 4}"))
             nc.scalar.activation(gd[:], d[c][:], ACT.Identity, bias=gain_col[:, c : c + 1], scale=1.0)
             return gd
 
-        def z_rows(tiles, gd, zt, first, count, banks):
-            for c in tiles:
-                nc.vector.tensor_tensor(
-                    h[c][:, first : first + count], pages[c % PAGES][:].indirect(entries(idx3, first, count)),
-                    gd[c][:, first : first + count], MULT,
+        def turn(bank, tiles, term, opens):
+            turns = [(i, c, k) for i, c in reversed(list(enumerate(tiles))) for k in range(BANK // (P * len(tiles)))]
+            for n, (i, c, k) in enumerate(turns):
+                place = (k * len(tiles) + i) * P
+                nc.tensor.matmul(
+                    bank[:, place : place + P], term[c][:, k * P : (k + 1) * P], ident[:],
+                    is_transpose=True, start=(opens and n == 0), stop=(not opens and n == len(turns) - 1),
                 )
-            step = count // len(banks)
+
+        def open_sum(tiles, first, number):
+            bank = bank_tile(number)
+            turn(bank, tiles, {c: d[c][:, first:] for c in tiles}, True)
+            return bank
+
+        def gather_rows(c, y, gd, first, count):
+            nc.vector.tensor_tensor(
+                y, pages[c % PAGES][:].indirect(entries(idx3, first, count)), gd[c][:, first : first + count], MULT
+            )
+
+        def close_sum(tiles, y, zt, first, bank):
+            turn(bank, tiles, y, False)
             rows = P * len(tiles)
             quarters = slice(32 * (tiles[0] % PACK), 32 * (tiles[-1] % PACK + 1))
-            for number, lo in zip(banks, range(first, first + count, step)):
-                bank = bank_tile(number)
-                turns = [(src, i, c, k) for src in (d, h) for i, c in enumerate(tiles) for k in range(step // P)]
-                for n, (src, i, c, k) in enumerate(turns):
-                    nc.tensor.matmul(
-                        bank[:, k * rows + i * P : k * rows + (i + 1) * P], src[c][:, lo + k * P : lo + (k + 1) * P], ident[:],
-                        is_transpose=True, start=(n == 0), stop=(n == len(turns) - 1),
+            for (start, width), tile in zt.items():
+                if first <= start < first + BANK // len(tiles):
+                    part = bank[:, (start - first) // P * rows : (start - first + width) // P * rows]
+                    nc.scalar.copy(
+                        tile[:, :, :, quarters, :], part.rearrange("m (k p u e) -> m k u p e", p=rows // PACK, u=2, e=2)
                     )
-                for (start, width), tile in zt.items():
-                    if lo <= start < lo + step:
-                        part = bank[:, (start - lo) // P * rows : (start - lo + width) // P * rows]
-                        nc.scalar.copy(
-                            tile[:, :, :, quarters, :], part.rearrange("m (k p u e) -> m k u p e", p=rows // PACK, u=2, e=2)
-                        )
 
-        def quantise_z(a, tile, first, count, banks, copy):
+        def quantise_z(a, tile, first, count, banks, copy, name):
             words = ring.tile([P, BANK, 2], F32, name="z_words", tag="raw", bufs=RAW_BUFS, align_bytes=64)
             step = count // len(banks)
             blocks = step // P
@@ -235,8 +243,11 @@ def tile_list_fibre_nonlinear_deinterleave_kernel(
                     words[:, lo : lo + step, :].rearrange("p (k m) u -> p k m u", m=P), turned.rearrange("p k u m -> p k m u")
                 )
             cols = slice(first, first + count)
+            codes = held([P, count], U32, name)
+            for lo in range(0, count, PIECE):
+                z_w[a, first + lo] = codes[:, lo : lo + PIECE]
             nc.vector.quantize_mx(
-                z_w[a][:, cols].bitcast(FP8X4), z_s[a][:, cols],
+                codes[:].bitcast(FP8X4), z_s[a][:, cols],
                 words[:, :count, :].rearrange("p m u -> p (m u)").bitcast(BF16),
             )
 
@@ -247,7 +258,7 @@ def tile_list_fibre_nonlinear_deinterleave_kernel(
                 nc.tensor.matmul_mx(
                     acc[:, k * PIECE : (k + 1) * PIECE],
                     w3_w[:, a, n0 : n0 + P].bitcast(FP8X4), w3_s[:, a, n0 : n0 + P],
-                    z_w[a][:, cols].bitcast(FP8X4), z_s[a][:, cols],
+                    z_w[a, first].bitcast(FP8X4), z_s[a][:, cols],
                     start=(start and k == 0), stop=(stop and k == 1),
                 )
 
@@ -255,11 +266,13 @@ def tile_list_fibre_nonlinear_deinterleave_kernel(
             out_rows = out[:, first : first + PIECE].rearrange("(k p) m -> p k m", p=P)
             nc.sync.dma_start(out_rows[:, 2 * half : 2 * half + 2, :], values.rearrange("p (k m) -> p k m", k=2))
 
-        gather_words(0, 0, S)
         for a in range(PASSES):
             nc.vector.tensor_copy(v_s[a][:], tab_s[:, a, :].indirect(idx1[:]))
+        ident = held([P, P], F32, "tab_s")
+        make_identity(nc, ident[:])
         quantise_sq(0)
         quantise_w2(0)
+        gather_words(0, 0, S)
         gather_words(1, 0, PIECE)
         def head_piece(c, piece, values):
             make_h(c, piece * PIECE, PIECE, (PAGES * piece + c) % 4, values)
@@ -273,8 +286,6 @@ def tile_list_fibre_nonlinear_deinterleave_kernel(
 
         head_piece(0, 0, piece_of(0, 0))
         gather_words(1, PIECE, S - PIECE)
-        pages.append(held([P, T2], F32, "tab_w1"))
-        nc.gpsimd.memset(pages[-1][:], 0.0)
         quantise_sq(1)
         head_piece(1, 0, spent("xn_last1"))
         head_piece(0, 1, piece_of(0, 1))
@@ -306,48 +317,75 @@ def tile_list_fibre_nonlinear_deinterleave_kernel(
         gd = {c: gain_plus_disp(c) for c in (0, 1, last)}
         quantise_w2(2)
         make_h_tile(3, (0, 1))
-        quantise_w2(3)
         zt = new_zt(0, [(0, BANK), (BANK, BANK)])
         for c in range(last - 1):
             pair = (2 * (c % 2), 2 * (c % 2) + 1)
             if c == PACK:
                 zt = new_zt(1, TAIL_PARTS)
-            z_rows([c], gd, zt, 0, M, pair)
+            gather_rows(c, h[c][:], gd, 0, M)
+            for half in range(2):
+                close_sum([c], {c: h[c][:, half * BANK :]}, zt, half * BANK, open_sum([c], half * BANK, pair[half]))
             if c > 0:
                 scatter_h(c + 2, 0, S, h[c + 2][:])
                 gd[c + 1] = gain_plus_disp(c + 1)
             if 0 < c <= last - 3:
                 make_h_tile(c + 3, pair)
+            if c == 1:
+                quantise_w2(3)
             if c == PACK - 1:
-                for (first, count), tile in zt.items():
-                    quantise_z(0, tile, first, count, (4, 5), nc.scalar.copy)
+                quantise_z(0, zt[BANK, BANK], BANK, BANK, (4, 5), nc.scalar.copy, "z_w0_late")
+                quantise_z(0, zt[0, BANK], 0, BANK, (4, 5), nc.scalar.copy, "z_w0_first")
         early, accs = {}, {}
-        for i in range(2):
-            early[i] = held([P, 2, BANK], F32, f"xn_last{i + 1}")
+        for i in (0, 2):
+            early[i] = held([P, 2, BANK], F32, f"xn_last{i // 2 + 1}")
             for half in range(2):
-                acc = bank_tile(4 + 2 * i + half)
+                acc = bank_tile(4 + i + half)
                 out_pass(0, i * PIECE, half, acc, True, True)
                 nc.scalar.copy(early[i][:, half, :], acc[:])
-        for i in range(2, 4):
+
+        def tail_rows(i):
+            y = {last - 1: h[last - 1][:, :PIECE] if i == 0 else y_put_off[:, (i - 1) * PIECE : i * PIECE]}
+            if i < 2:
+                y[last] = y_last[:, i * PIECE : (i + 1) * PIECE]
+            else:
+                y[last] = y_end[:, (i - 2) * PIECE : (i - 1) * PIECE]
+            for c in (last - 1, last):
+                gather_rows(c, y[c], gd, i * PIECE, PIECE)
+            close_sum([last - 1, last], y, zt, i * PIECE, sums[i])
+
+        def tail_codes(i):
+            quantise_z(1, zt[i * PIECE, PIECE], i * PIECE, PIECE, (i,), nc.scalar.copy, f"z_w1_{i}")
+
+        def finish_out(i):
             for half in range(2):
-                accs[i, half] = bank_tile(2 * i + half)
+                if i % 2:
+                    out_pass(1, i * PIECE, half, accs[i, half], False, True)
+                    staged = ring.tile([P, BANK], F32, name="staged", tag="raw", bufs=RAW_BUFS, align_bytes=64)
+                    copy = nc.vector.tensor_copy if (i, half) == (3, 1) else nc.scalar.copy
+                    copy(staged[:], accs[i, half][:])
+                    store_out(i * PIECE, half, staged[:])
+                else:
+                    acc = bank_tile(i + half)
+                    out_pass(1, i * PIECE, half, acc, True, True)
+                    nc.vector.tensor_tensor(early[i][:, half, :], acc[:], early[i][:, half, :], ADD)
+                    store_out(i * PIECE, half, early[i][:, half, :])
+
+        for i in (1, 3):
+            for half in range(2):
+                accs[i, half] = bank_tile(3 + i + half)
                 out_pass(0, i * PIECE, half, accs[i, half], True, False)
-        for i in range(5):
-            if i < 4:
-                z_rows([last - 1, last], gd, zt, i * PIECE, PIECE, (i,))
-            if i > 0:
-                first = (i - 1) * PIECE
-                quantise_z(1, zt[first, PIECE], first, PIECE, (i - 1,), nc.vector.tensor_copy if i == 2 else nc.scalar.copy)
-        for i in range(2):
-            for half in range(2):
-                acc = bank_tile(2 * i + half)
-                out_pass(1, i * PIECE, half, acc, True, True)
-                nc.vector.tensor_tensor(early[i][:, half, :], acc[:], early[i][:, half, :], ADD)
-                store_out(i * PIECE, half, early[i][:, half, :])
-        for i in range(2, 4):
-            for half in range(2):
-                out_pass(1, i * PIECE, half, accs[i, half], False, True)
-                staged = ring.tile([P, BANK], F32, name="staged", tag="raw", bufs=RAW_BUFS, align_bytes=64)
-                copy = nc.vector.tensor_copy if (i, half) == (3, 1) else nc.scalar.copy
-                copy(staged[:], accs[i, half][:])
-                store_out(i * PIECE, half, staged[:])
+        sums = [open_sum([last - 1, last], i * PIECE, i) for i in range(4)]
+        y_put_off = held([P, M - PIECE], F32, f"d{last - 1}")
+        y_last = held([P, 2 * PIECE], F32, f"d{last}")
+        tail_rows(0)
+        tail_rows(1)
+        tail_codes(0)
+        y_end = held([P, 2 * PIECE], F32, "zt1_0")
+        tail_rows(2)
+        tail_codes(1)
+        tail_rows(3)
+        finish_out(0)
+        tail_codes(2)
+        tail_codes(3)
+        for i in range(1, 4):
+            finish_out(i)

@@ -24,11 +24,10 @@ K_PASS = P * PACK
 PASSES = K // K_PASS
 BANK = 512
 PIECE = 256
-ROW_TILES = H // P
+PIECES = M // PIECE
 PER_COL = 16
-RAW_BUFS = 8
 PAGES = 3
-TAIL_PARTS = [(first, PIECE) for first in range(0, M, PIECE)]
+KIB = 1024
 
 
 def tile_list_fibre_nonlinear_deinterleave_kernel(
@@ -37,7 +36,8 @@ def tile_list_fibre_nonlinear_deinterleave_kernel(
     nc = tc.nc
     with ExitStack() as ctx:
         keep = ctx.enter_context(tc.tile_pool(name="keep", bufs=1))
-        ring = ctx.enter_context(tc.tile_pool(name="ring", bufs=2))
+        ring = ctx.enter_context(tc.tile_pool(name="ring", bufs=3))
+        laid = ctx.enter_context(tc.tile_pool(name="laid", bufs=1))
         psum = ctx.enter_context(tc.psum_pool(name="psum", bufs=1))
 
         def bank_tile(number):
@@ -46,41 +46,51 @@ def tile_list_fibre_nonlinear_deinterleave_kernel(
         def held(shape, dtype, name):
             return keep.tile(shape, dtype, name=name, align_bytes=64)
 
+        def placed(shape, dtype, name, kib):
+            return laid.tile(shape, dtype, name=name, align_bytes=64, offset=kib * KIB)
+
         idx1 = held([P, S // PER_COL], U16, "idx1")
         idx2 = held([P, S // PER_COL], U16, "idx2")
         idx3 = held([P, M // PER_COL], U16, "idx3")
-        tab_w = [held([P, T], I32, f"tab_w{a}") for a in range(PASSES)]
+        tab_w = [placed([P, T], I32, f"tab_w{a}", 48 + 8 * a) for a in range(PASSES)]
         tab_s = held([P, PASSES, T], U8, "tab_s")
         v_w = [held([P, S], U32, f"v_w{a}") for a in range(PASSES)]
         v_s = [held([P, S], U8, f"v_s{a}") for a in range(PASSES)]
-        w1_head = held([P, PASSES, 2 * PIECE], U8, "w1_head")
-        w1_rest = held([P, PASSES, 2 * (H - PIECE)], U8, "w1_rest")
+        w1_early = [held([P, PASSES, 2 * PIECE], U8, f"w1_early{i}") for i in range(2)]
+        w1_late = held([P, PASSES, K_PASS], U16, "w1_late")
+        w1_dealt = held([P, PASSES, PACK, P], U16, "w1_dealt")
         w1_s = held([P, PASSES, H], U8, "w1_s")
+        w1_s_dealt = held([P, PASSES, PACK, P], U8, "w1_s_dealt")
         w3_w = held([P, PASSES, N], I32, "w3_w")
         w3_s = held([P, PASSES, N], U8, "w3_s")
         sq_w = [held([P, S], U32, f"sq_w{a}") for a in range(PASSES)]
         sq_s = [held([P, S], U8, f"sq_s{a}") for a in range(PASSES)]
-        w2_w = [held([P, PASSES, PIECE], U32, f"w2_w{piece}") for piece in range(H // PIECE)]
-        w2_s = [held([P, PASSES, PIECE], U8, f"w2_s{piece}") for piece in range(H // PIECE)]
+        w2_w = [held([P, PASSES, PIECE], U32, f"w2_w{i}") for i in range(2)]
+        w2_s = [held([P, PASSES, PIECE], U8, f"w2_s{i}") for i in range(2)]
+        w2_w_dealt = [held([P, K_PASS], U32, f"w2_w_dealt{a}") for a in range(PASSES)]
+        w2_s_dealt = [held([P, K_PASS], U8, f"w2_s_dealt{a}") for a in range(PASSES)]
         z_w = {}
         z_s = [held([P, M], U8, f"z_s{a}") for a in range(PASSES)]
         weights = held([P, S], F32, "weights")
         pages = [held([P, T2], F32, f"page{i}") for i in range(PAGES)]
-        gain_rows = held([P, P], F32, "gain_rows")
-        gain_col = held([P, ROW_TILES], F32, "gain_col")
-        h = {c: held([P, S], F32, f"h{c}") for c in range(PAGES)}
-        d = [held([P, M], F32, f"d{c}") for c in range(ROW_TILES)]
+        gain_early = held([P, PACK], F32, "gain_early")
+        gain_dealt = held([P, PACK], F32, "gain_dealt")
+        h = {0: held([P, S], F32, "h0")}
+        d_early = [held([P, M], F32, f"d{c}") for c in range(PACK)]
+        d_pair = [placed([P, 2, M], F32, "d45", 40), held([P, 2, M], F32, "d67")]
+        w2_late = [placed([P, PACK, K_PASS], F32, f"w2_late{a}", 19 + 8 * a) for a in range(PASSES)]
+        d = {c: d_early[c][:] for c in range(PACK)}
+        d.update({PACK + t: d_pair[t // 2][:, t % 2, :] for t in range(PACK)})
 
         nc.gpsimd.memset(tab_s[:].rearrange("p a t -> p (a t)").bitcast(I32), 0)
         nc.vector.memset(w1_s[:].rearrange("p a t -> p (a t)").bitcast(I32), 0)
         for page in pages:
             nc.vector.memset(page[:], 0.0)
         nc.vector.memset(w3_s[:].rearrange("p a t -> p (a t)").bitcast(I32), 0)
-        nc.vector.memset(gain_rows[:], 0.0)
 
-        def load_scale_rows(queue, plane, scales):
+        def load_scale_rows(plane, scales):
             for r in range(4):
-                queue.dma_start(
+                nc.sync.dma_start(
                     plane[r:P:32, :, :].bitcast(I32),
                     scales[:, r:16:4, :].rearrange("a q n -> q a n").bitcast(I32),
                 )
@@ -88,54 +98,68 @@ def tile_list_fibre_nonlinear_deinterleave_kernel(
         def load_table_words(a):
             nc.sync.dma_start(tab_w[a][:], tab_words[a].rearrange("p t i -> p (t i)").bitcast(I32))
 
-        def load_rows(matrix, a, piece):
-            if matrix is xn and a == PASSES - 1 and piece > 0:
-                raw = held([P, PACK, PIECE], F32, f"xn_last{piece}")
-            elif a == PASSES - 1 and piece == 1:
-                raw = held([P, PACK, PIECE], F32, "w2_last")
+        def load_rows(matrix, a, piece, name):
+            if piece == 0:
+                raw = placed([P, PACK, PIECE], F32, name, 4 * a + (0 if matrix is xn else 8))
             else:
-                raw = ring.tile([P, PACK, PIECE], F32, name="raw", tag="raw", bufs=RAW_BUFS, align_bytes=64)
+                raw = held([P, PACK, PIECE], F32, name)
             rows = matrix[a * K_PASS : (a + 1) * K_PASS, piece * PIECE : (piece + 1) * PIECE]
             nc.sync.dma_start(raw[:], rows.rearrange("(p t) w -> p t w", t=PACK))
             return raw
 
-        def load_disp(c):
-            nc.sync.dma_start(d[c][:], disp[c * P : (c + 1) * P, :])
-
         w1_bytes = w1_words.rearrange("a p n -> p a n")
         xn_raw, w2_raw = {}, {}
-        load_scale_rows(nc.sync, tab_s, tab_scales)
+        load_scale_rows(tab_s, tab_scales)
         nc.sync.dma_start(idx1[:], offs)
         nc.sync.dma_start(idx2[:], offs2)
         nc.sync.dma_start(idx3[:], offs3)
-        nc.sync.dma_start(w1_head[:].bitcast(I32), w1_bytes[:, :, : 2 * PIECE].bitcast(I32))
+        nc.sync.dma_start(w1_early[0][:].bitcast(I32), w1_bytes[:, :, : 2 * PIECE].bitcast(I32))
         for a in range(PASSES):
-            xn_raw[a, 0] = load_rows(xn, a, 0)
+            xn_raw[a, 0] = load_rows(xn, a, 0, f"raw{a}")
         for a in range(PASSES):
-            w2_raw[a, 0] = load_rows(w2, a, 0)
+            w2_raw[a, 0] = load_rows(w2, a, 0, f"raw{2 + a}")
         load_table_words(0)
-        load_scale_rows(nc.sync, w1_s, w1_scales)
+        load_scale_rows(w1_s, w1_scales)
         load_table_words(1)
         nc.sync.dma_start(weights[:, :PIECE], wgs[:, :PIECE])
-        for a in range(PASSES):
-            xn_raw[a, 1] = load_rows(xn, a, 1)
+        xn_raw[0, 1] = load_rows(xn, 0, 1, "raw4")
+        xn_raw[1, 1] = load_rows(xn, 1, 1, "xn_last1")
         nc.sync.dma_start(weights[:, PIECE:], wgs[:, PIECE:])
-        for a in range(PASSES):
-            w2_raw[a, 1] = load_rows(w2, a, 1)
-        nc.sync.dma_start(w1_rest[:].bitcast(I32), w1_bytes[:, :, 2 * PIECE :].bitcast(I32))
+        w2_raw[0, 1] = load_rows(w2, 0, 1, "raw5")
+        w2_raw[1, 1] = load_rows(w2, 1, 1, "w2_last")
+        nc.sync.dma_start(w1_early[1][:].bitcast(I32), w1_bytes[:, :, 2 * PIECE : 4 * PIECE].bitcast(I32))
         for piece in (2, 3):
-            for a in range(PASSES):
-                xn_raw[a, piece] = load_rows(xn, a, piece)
-        nc.sync.dma_start(gain_rows[:ROW_TILES, :], gain.rearrange("(c p) -> c p", p=P))
-        for tiles, piece in ((range(0, 2), 2), (range(2, 3), 3)):
-            for c in tiles:
-                load_disp(c)
-            for a in range(PASSES):
-                w2_raw[a, piece] = load_rows(w2, a, piece)
-        for c in range(3, ROW_TILES):
-            load_disp(c)
+            xn_raw[0, piece] = load_rows(xn, 0, piece, f"raw{4 + piece}")
+            xn_raw[1, piece] = load_rows(xn, 1, piece, f"xn_last{piece}")
+        with nc.allow_non_contiguous_dma(reason="one gain a partition"):
+            nc.sync.dma_start(gain_early[:], gain[:K_PASS].rearrange("(c p) -> p c", p=P))
+        nc.sync.dma_start(gain_dealt[:], gain[K_PASS:].rearrange("(p t) -> p t", t=PACK))
+        nc.sync.dma_start(d[0], disp[:P, :])
+        weights_dealt = [placed([P, S], F32, f"weights_dealt{t}", 4 * t) for t in range(PACK)]
+
+        def load_weights_dealt(t):
+            for q in range(4):
+                nc.sync.dma_start(weights_dealt[t][32 * q : 32 * (q + 1), :], wgs[t:P:PACK, :])
+
+        def load_w2_late(a):
+            rows = w2[a * K_PASS : (a + 1) * K_PASS, K_PASS:]
+            nc.sync.dma_start(w2_late[a][:], rows.rearrange("(p t) w -> p t w", t=PACK))
+
+        load_w2_late(0)
+        load_weights_dealt(0)
+        load_w2_late(1)
+        nc.sync.dma_start(d[1], disp[P : 2 * P, :])
+        nc.sync.dma_start(w1_late[:].bitcast(I32), w1_bytes[:, :, 2 * K_PASS :].bitcast(I32))
+        nc.sync.dma_start(d[2], disp[2 * P : 3 * P, :])
+        late_rows = disp[K_PASS:, :].rearrange("(p t) m -> p t m", t=PACK)
+        load_weights_dealt(1)
+        nc.sync.dma_start(d[3], disp[3 * P : 4 * P, :])
+        nc.sync.dma_start(d_pair[0][:], late_rows[:, 0:2, :])
+        load_weights_dealt(2)
+        nc.sync.dma_start(d_pair[1][:], late_rows[:, 2:4, :])
+        load_weights_dealt(3)
         nc.sync.dma_start(w3_w[:], w3_words.rearrange("a p n i -> p a (n i)").bitcast(I32))
-        load_scale_rows(nc.sync, w3_s, w3_scales)
+        load_scale_rows(w3_s, w3_scales)
 
         def interleave(grouped, raw, func):
             nc.scalar.activation(
@@ -145,12 +169,12 @@ def tile_list_fibre_nonlinear_deinterleave_kernel(
         def quantise_sq(piece):
             cols = slice(piece * PIECE, (piece + 1) * PIECE)
             for a in range(PASSES):
-                grouped = ring.tile([P, PIECE, PACK], BF16, name="sq_grouped", bufs=3, align_bytes=64)
+                grouped = ring.tile([P, PIECE, PACK], BF16, name="sq_grouped", align_bytes=64)
                 interleave(grouped[:], xn_raw[a, piece], ACT.Square)
                 nc.vector.quantize_mx(sq_w[a][:, cols].bitcast(FP8X4), sq_s[a][:, cols], grouped[:].rearrange("p w t -> p (w t)"))
 
         def quantise_w2(piece):
-            grouped = held([P, PASSES, PIECE, PACK], BF16, ("w2_grouped0", "w2_grouped1", "xn_last3", "tab_w0")[piece])
+            grouped = held([P, PASSES, PIECE, PACK], BF16, f"w2_grouped{piece}")
             for a in range(PASSES):
                 interleave(grouped[:, a, :, :], w2_raw[a, piece], ACT.Copy)
             nc.vector.quantize_mx(
@@ -159,112 +183,101 @@ def tile_list_fibre_nonlinear_deinterleave_kernel(
                 grouped[:].rearrange("p a w t -> p (a w t)"),
             )
 
+        def quantise_w2_dealt(a):
+            grouped = held([P, PACK, P, PACK], BF16, f"w2_grouped{a}")
+            nc.scalar.activation(
+                grouped[:].rearrange("p t m j -> p m t j"), w2_late[a][:].rearrange("p j (m t) -> p m t j", t=PACK), ACT.Copy
+            )
+            nc.vector.quantize_mx(w2_w_dealt[a][:].bitcast(FP8X4), w2_s_dealt[a][:], grouped[:].rearrange("p t m j -> p (t m j)"))
+
         def entries(idx, first, count):
             return idx[:, first // PER_COL : (first + count) // PER_COL]
 
         def gather_words(a, first, count):
             nc.vector.tensor_copy(v_w[a][:, first : first + count], tab_w[a][:].bitcast(U32).indirect(entries(idx1, first, count)))
 
+        def stationary(c, a):
+            if c < PACK:
+                piece, first = divmod(c * P, PIECE)
+                cols = slice(first, first + P)
+                return (
+                    w2_w[piece][:, a, cols], w2_s[piece][:, a, cols],
+                    w1_early[piece][:, a, 2 * first : 2 * (first + P)], w1_s[:, a, c * P : (c + 1) * P],
+                )
+            t = c - PACK
+            cols = slice(t * P, (t + 1) * P)
+            return w2_w_dealt[a][:, cols], w2_s_dealt[a][:, cols], w1_dealt[:, a, t, :].bitcast(U8), w1_s_dealt[:, a, t, :]
+
         def make_h(c, first, count, number, values):
             acc = bank_tile(number)
-            rows = slice(c * P, (c + 1) * P)
-            piece, w2_first = divmod(c * P, PIECE)
-            w2_cols = slice(w2_first, w2_first + P)
             cols = slice(first, first + count)
             for a in range(PASSES):
+                codes, scales, unused_codes, unused_scales = stationary(c, a)
                 nc.tensor.matmul_mx(
-                    acc[:, :count], w2_w[piece][:, a, w2_cols].bitcast(FP8X4), w2_s[piece][:, a, w2_cols],
+                    acc[:, :count], codes.bitcast(FP8X4), scales,
                     sq_w[a][:, cols].bitcast(FP8X4), sq_s[a][:, cols], start=(a == 0), stop=False,
                 )
-            width = BANK if count == BANK else P
-            w1_tile, w1_first = (w1_head, c * P) if c * P < PIECE else (w1_rest, c * P - PIECE)
             for a in range(PASSES):
-                for lo in range(0, count, width):
-                    part = slice(first + lo, first + lo + width)
-                    nc.tensor.matmul_mx(
-                        acc[:, lo : lo + width], w1_tile[:, a, 2 * w1_first : 2 * (w1_first + P)].bitcast(FP4X4), w1_s[:, a, rows],
-                        v_w[a][:, part].bitcast(FP8X4), v_s[a][:, part],
-                        start=False, stop=(a == PASSES - 1 and lo + width == count),
-                    )
+                unused_codes, unused_scales, codes, scales = stationary(c, a)
+                nc.tensor.matmul_mx(
+                    acc[:, :count], codes.bitcast(FP4X4), scales,
+                    v_w[a][:, cols].bitcast(FP8X4), v_s[a][:, cols], start=False, stop=(a == PASSES - 1),
+                )
             nc.scalar.activation(values, acc[:, :count], ACT.Tanh)
 
         def scatter_h(c, first, count, values):
             cols = slice(first, first + count)
-            nc.vector.tensor_tensor(pages[c % PAGES][:].indirect(entries(idx2, first, count)), values, weights[:, cols], MULT)
+            factor = weights[:, cols] if c < PACK else weights_dealt[c - PACK][:, cols]
+            nc.vector.tensor_tensor(pages[c % PAGES][:].indirect(entries(idx2, first, count)), values, factor, MULT)
 
-        def gain_plus_disp(c):
-            gd = held([P, M], F32, {0: "tab_w0", 1: "tab_w1", 6: "gd6", 7: "gd7"}.get(c, f"h{(c - 1) % 4}"))
-            nc.scalar.activation(gd[:], d[c][:], ACT.Identity, bias=gain_col[:, c : c + 1], scale=1.0)
+        def gain_plus_disp(c, gd):
+            bias = gain_early[:, c : c + 1] if c < PACK else gain_dealt[:, c - PACK : c - PACK + 1]
+            nc.scalar.activation(gd[:], d[c], ACT.Identity, bias=bias, scale=1.0)
             return gd
 
-        def turn(bank, tiles, term, opens):
-            turns = [(i, c, k) for i, c in reversed(list(enumerate(tiles))) for k in range(BANK // (P * len(tiles)))]
-            for n, (i, c, k) in enumerate(turns):
-                place = (k * len(tiles) + i) * P
-                nc.tensor.matmul(
-                    bank[:, place : place + P], term[c][:, k * P : (k + 1) * P], ident[:],
-                    is_transpose=True, start=(opens and n == 0), stop=(not opens and n == len(turns) - 1),
+        def gather_rows(c, y, gd, first, count):
+            nc.vector.tensor_tensor(y, pages[c % PAGES][:].indirect(entries(idx3, first, count)), gd[:, first : first + count], MULT)
+
+        def turn(bank, place, term, start, stop):
+            nc.tensor.matmul(bank[:, place * P : (place + 1) * P], term, ident[:], is_transpose=True, start=start, stop=stop)
+
+        def turn_tile(c, y, zt, banks):
+            for half in range(2):
+                bank = bank_tile(banks[half])
+                for n, term in enumerate((d[c], y)):
+                    for k in range(4):
+                        first = half * BANK + k * P
+                        turn(bank, k, term[:, first : first + P], n == 0 and k == 0, n == 1 and k == 3)
+                nc.scalar.copy(
+                    zt[half][:, :, :, 32 * c : 32 * (c + 1), :], bank[:].rearrange("m (k p u e) -> m k u p e", p=32, u=2, e=2)
                 )
 
-        def open_sum(tiles, first, number):
-            bank = bank_tile(number)
-            turn(bank, tiles, {c: d[c][:, first:] for c in tiles}, True)
-            return bank
-
-        def gather_rows(c, y, gd, first, count):
-            nc.vector.tensor_tensor(
-                y, pages[c % PAGES][:].indirect(entries(idx3, first, count)), gd[c][:, first : first + count], MULT
-            )
-
-        def close_sum(tiles, y, zt, first, bank):
-            turn(bank, tiles, y, False)
-            rows = P * len(tiles)
-            quarters = slice(32 * (tiles[0] % PACK), 32 * (tiles[-1] % PACK + 1))
-            for (start, width), tile in zt.items():
-                if first <= start < first + BANK // len(tiles):
-                    part = bank[:, (start - first) // P * rows : (start - first + width) // P * rows]
-                    nc.scalar.copy(
-                        tile[:, :, :, quarters, :], part.rearrange("m (k p u e) -> m k u p e", p=rows // PACK, u=2, e=2)
-                    )
-
-        def quantise_z(a, tile, first, count, banks, copy, name):
-            words = ring.tile([P, BANK, 2], F32, name="z_words", tag="raw", bufs=RAW_BUFS, align_bytes=64)
-            step = count // len(banks)
-            blocks = step // P
-            for number, lo in zip(banks, range(0, count, step)):
+        def quantise_z0(half, zt, codes):
+            words = placed([P, BANK, 2], F32, f"z0_words{half}", 16 + 4 * half)
+            for n, number in enumerate((4, 5)):
                 bank = bank_tile(number)
-                turned = bank[:, : 2 * step].rearrange("p (k u m) -> p k u m", u=2, m=P)
-                for k in range(blocks):
+                turned = bank[:].rearrange("p (k u m) -> p k u m", u=2, m=P)
+                for k in range(2):
                     for u in range(2):
                         nc.tensor.transpose(
-                            turned[:, k, u, :], tile[:, lo // P + k, u, :, :].rearrange("m p e -> m (p e)").bitcast(F32), ident[:]
+                            turned[:, k, u, :], zt[:, 2 * n + k, u, :, :].rearrange("m p e -> m (p e)").bitcast(F32), ident[:]
                         )
-                copy(
-                    words[:, lo : lo + step, :].rearrange("p (k m) u -> p k m u", m=P), turned.rearrange("p k u m -> p k m u")
+                nc.scalar.copy(
+                    words[:, n * PIECE : (n + 1) * PIECE, :].rearrange("p (k m) u -> p k m u", m=P), turned.rearrange("p k u m -> p k m u")
                 )
-            cols = slice(first, first + count)
-            codes = held([P, count], U32, name)
-            for lo in range(0, count, PIECE):
-                z_w[a, first + lo] = codes[:, lo : lo + PIECE]
-            nc.vector.quantize_mx(
-                codes[:].bitcast(FP8X4), z_s[a][:, cols],
-                words[:, :count, :].rearrange("p m u -> p (m u)").bitcast(BF16),
-            )
+            cols = slice(half * BANK, (half + 1) * BANK)
+            nc.vector.quantize_mx(codes[:, cols].bitcast(FP8X4), z_s[0][:, cols], words[:].rearrange("p m u -> p (m u)").bitcast(BF16))
 
-        def out_pass(a, first, half, acc, start, stop):
-            cols = slice(first, first + PIECE)
+        def out_pass(a, i, half, acc):
+            cols = slice(i * PIECE, (i + 1) * PIECE)
             for k in range(2):
                 n0 = (2 * half + k) * P
                 nc.tensor.matmul_mx(
                     acc[:, k * PIECE : (k + 1) * PIECE],
                     w3_w[:, a, n0 : n0 + P].bitcast(FP8X4), w3_s[:, a, n0 : n0 + P],
-                    z_w[a, first].bitcast(FP8X4), z_s[a][:, cols],
-                    start=(start and k == 0), stop=(stop and k == 1),
+                    z_w[a, i].bitcast(FP8X4), z_s[a][:, cols],
+                    start=(a == 0 and k == 0), stop=(a == 1 and k == 1),
                 )
-
-        def store_out(first, half, values):
-            out_rows = out[:, first : first + PIECE].rearrange("(k p) m -> p k m", p=P)
-            nc.sync.dma_start(out_rows[:, 2 * half : 2 * half + 2, :], values.rearrange("p (k m) -> p k m", k=2))
 
         for a in range(PASSES):
             nc.vector.tensor_copy(v_s[a][:], tab_s[:, a, :].indirect(idx1[:]))
@@ -273,7 +286,9 @@ def tile_list_fibre_nonlinear_deinterleave_kernel(
         quantise_sq(0)
         quantise_w2(0)
         gather_words(0, 0, S)
+        nc.vector.tensor_copy(w1_s_dealt[:], w1_s[:, :, K_PASS:].rearrange("p a (m t) -> p a t m", t=PACK))
         gather_words(1, 0, PIECE)
+
         def head_piece(c, piece, values):
             make_h(c, piece * PIECE, PIECE, (PAGES * piece + c) % 4, values)
             scatter_h(c, piece * PIECE, PIECE, values)
@@ -286,6 +301,8 @@ def tile_list_fibre_nonlinear_deinterleave_kernel(
 
         head_piece(0, 0, piece_of(0, 0))
         gather_words(1, PIECE, S - PIECE)
+        middle = {1: 50, 2: 58, 3: 34}
+        h.update({c: placed([P, S], F32, f"h{c}", middle[c]) for c in (1, 2)})
         quantise_sq(1)
         head_piece(1, 0, spent("xn_last1"))
         head_piece(0, 1, piece_of(0, 1))
@@ -299,93 +316,114 @@ def tile_list_fibre_nonlinear_deinterleave_kernel(
                 head_piece(c, piece, piece_of(c, piece))
         head_piece(2, 3, piece_of(2, 3))
 
-        def make_h_tile(c, banks):
-            h[c] = held([P, S], F32, f"h{c % 4}")
+        def make_h_tile(c, values):
+            h[c] = values
             for half in range(2):
-                make_h(c, half * BANK, BANK, banks[half], h[c][:, half * BANK : (half + 1) * BANK])
+                make_h(c, half * BANK, BANK, 6 + half, values[:, half * BANK : (half + 1) * BANK])
 
-        gain_bank = bank_tile(6)
-        nc.tensor.transpose(gain_bank[:, :P], gain_rows[:], ident[:])
-        nc.scalar.copy(gain_col[:], gain_bank[:, :ROW_TILES])
+        gd = {0: gain_plus_disp(0, held([P, M], F32, "gd0"))}
+        for a in range(PASSES):
+            quantise_w2_dealt(a)
+        gd[1] = gain_plus_disp(1, held([P, M], F32, "gd1"))
+        make_h_tile(3, placed([P, S], F32, "h3", middle[3]))
+        nc.scalar.copy(w1_dealt[:], w1_late[:].rearrange("p a (m t) -> p a t m", t=PACK))
 
-        def new_zt(a, parts):
-            return {
-                (first, count): held([P, count // P, 2, P, 2], BF16, f"zt{a}_{first}") for first, count in parts
-            }
-
-        last = ROW_TILES - 1
-        gd = {c: gain_plus_disp(c) for c in (0, 1, last)}
-        quantise_w2(2)
-        make_h_tile(3, (0, 1))
-        zt = new_zt(0, [(0, BANK), (BANK, BANK)])
-        for c in range(last - 1):
-            pair = (2 * (c % 2), 2 * (c % 2) + 1)
-            if c == PACK:
-                zt = new_zt(1, TAIL_PARTS)
-            gather_rows(c, h[c][:], gd, 0, M)
-            for half in range(2):
-                close_sum([c], {c: h[c][:, half * BANK :]}, zt, half * BANK, open_sum([c], half * BANK, pair[half]))
+        zt = [placed([P, 4, 2, P, 2], BF16, f"zt{half}", 28 - 4 * half) for half in range(2)]
+        for c in range(PACK):
+            gather_rows(c, h[c][:], gd[c], 0, M)
+            turn_tile(c, h[c][:], zt, (2 * (c % 2), 2 * (c % 2) + 1))
             if c > 0:
                 scatter_h(c + 2, 0, S, h[c + 2][:])
-                gd[c + 1] = gain_plus_disp(c + 1)
-            if 0 < c <= last - 3:
-                make_h_tile(c + 3, pair)
-            if c == 1:
-                quantise_w2(3)
-            if c == PACK - 1:
-                quantise_z(0, zt[BANK, BANK], BANK, BANK, (4, 5), nc.scalar.copy, "z_w0_late")
-                quantise_z(0, zt[0, BANK], 0, BANK, (4, 5), nc.scalar.copy, "z_w0_first")
-        early, accs = {}, {}
-        for i in (0, 2):
-            early[i] = held([P, 2, BANK], F32, f"xn_last{i // 2 + 1}")
-            for half in range(2):
-                acc = bank_tile(4 + i + half)
-                out_pass(0, i * PIECE, half, acc, True, True)
-                nc.scalar.copy(early[i][:, half, :], acc[:])
+                gd[c + 1] = gain_plus_disp(c + 1, placed([P, M], F32, f"gd{c + 1}", middle[c] + (2 if c == 3 else -2)))
+                make_h_tile(c + 3, placed([P, S], F32, f"h{c + 3}", middle[c] + (-2 if c == 3 else 2)))
 
-        def tail_rows(i):
-            y = {last - 1: h[last - 1][:, :PIECE] if i == 0 else y_put_off[:, (i - 1) * PIECE : i * PIECE]}
-            if i < 2:
-                y[last] = y_last[:, i * PIECE : (i + 1) * PIECE]
-            else:
-                y[last] = y_end[:, (i - 2) * PIECE : (i - 1) * PIECE]
-            for c in (last - 1, last):
-                gather_rows(c, y[c], gd, i * PIECE, PIECE)
-            close_sum([last - 1, last], y, zt, i * PIECE, sums[i])
+        sums = [bank_tile(i) for i in range(PIECES)]
+
+        def turn_pair(e, term, opens, closes):
+            for i in range(PIECES):
+                for k in range(2):
+                    first = i * PIECE + k * P
+                    turn(sums[i], 2 * k + e, term[:, first : first + P], opens and k == 0, closes and k == 1)
+
+        turn_pair(0, d[4], True, False)
+        turn_pair(1, d[5], False, False)
+        gather_rows(4, h[4][:], gd[4], 0, M)
+        turn_pair(0, h[4][:], False, False)
+        scatter_h(6, 0, S, h[6][:])
+        gd[5] = gain_plus_disp(5, placed([P, M], F32, "gd5", middle[1] + 2))
+        codes0 = placed([P, M], U32, "codes0", middle[2] + 2)
+        for half in range(2):
+            quantise_z0(half, zt[half], codes0)
+        for i in range(PIECES):
+            z_w[0, i] = codes0[:, i * PIECE : (i + 1) * PIECE]
+        y5 = held([P, M], F32, "h0")
+        gather_rows(5, y5[:], gd[5], 0, M)
+        gd[6] = gain_plus_disp(6, placed([P, M], F32, "gd6", 40))
+        make_h_tile(7, placed([P, S], F32, "h7", 44))
+        turn_pair(1, y5[:], False, True)
+        y_pair = [held([P, 2, PIECE], F32, name) for name in ("xn_last1", "xn_last2", "xn_last3", "w2_last")]
+        for i in range(PIECES):
+            gather_rows(6, y_pair[i][:, 0, :], gd[6], i * PIECE, PIECE)
+        scatter_h(7, 0, S, h[7][:])
+
+        halves = [held([P, 2, PIECE], F32, f"d{i}") for i in range(PIECES)]
+        turned_pair = []
+        for i in range(PIECES):
+            turned_pair.append(held([P, 2, P, 2], BF16, f"turned_pair{i}"))
+            nc.scalar.copy(turned_pair[i][:], sums[i][:].rearrange("m (k e p) -> m k p e", k=2, e=2))
+        for n in range(2):
+            bank = bank_tile(4 + n)
+            for place in range(4):
+                i, k = 2 * n + place // 2, place % 2
+                nc.tensor.transpose(
+                    bank[:, place * P : (place + 1) * P], turned_pair[i][:, k, :, :].rearrange("m p e -> m (p e)").bitcast(F32), ident[:]
+                )
+            for i in (2 * n, 2 * n + 1):
+                nc.scalar.copy(halves[i][:, 0, :], bank[:, (i % 2) * PIECE : (i % 2 + 1) * PIECE])
+        gd[7] = gain_plus_disp(7, held([P, M], F32, "h0"))
+        accs = {}
+        for i in range(PIECES):
+            for half in range(2):
+                accs[i, half] = bank_tile((6 + 2 * i + half) % 8)
+                out_pass(0, i, half, accs[i, half])
+
+        def pair_sum(i):
+            nc.vector.tensor_tensor(
+                halves[i][:, 1, :].bitcast(BF16).rearrange("p (m e) -> p m e", e=2),
+                y_pair[i][:].rearrange("p e m -> p m e"),
+                d_pair[1][:, :, i * PIECE : (i + 1) * PIECE].rearrange("p e m -> p m e"),
+                ADD,
+            )
+
+        woven = [held([P, PIECE, 2], F32, f"raw{4 + i}") for i in range(PIECES)]
+
+        def weave(i):
+            copy = nc.scalar.copy if i < 2 else nc.vector.tensor_copy
+            copy(woven[i][:], halves[i][:].rearrange("p u m -> p m u"))
 
         def tail_codes(i):
-            quantise_z(1, zt[i * PIECE, PIECE], i * PIECE, PIECE, (i,), nc.scalar.copy, f"z_w1_{i}")
+            words = woven[i]
+            codes = held([P, PIECE], U32, f"z_w1_{i}")
+            z_w[1, i] = codes[:]
+            nc.vector.quantize_mx(
+                codes[:].bitcast(FP8X4), z_s[1][:, i * PIECE : (i + 1) * PIECE], words[:].rearrange("p m u -> p (m u)").bitcast(BF16)
+            )
 
         def finish_out(i):
+            staged = placed([P, 2, BANK], F32, f"staged{i}", 16 + 4 * i)
+            out_rows = out[:, i * PIECE : (i + 1) * PIECE].rearrange("(k p) m -> p k m", p=P)
             for half in range(2):
-                if i % 2:
-                    out_pass(1, i * PIECE, half, accs[i, half], False, True)
-                    staged = ring.tile([P, BANK], F32, name="staged", tag="raw", bufs=RAW_BUFS, align_bytes=64)
-                    copy = nc.vector.tensor_copy if (i, half) == (3, 1) else nc.scalar.copy
-                    copy(staged[:], accs[i, half][:])
-                    store_out(i * PIECE, half, staged[:])
-                else:
-                    acc = bank_tile(i + half)
-                    out_pass(1, i * PIECE, half, acc, True, True)
-                    nc.vector.tensor_tensor(early[i][:, half, :], acc[:], early[i][:, half, :], ADD)
-                    store_out(i * PIECE, half, early[i][:, half, :])
+                out_pass(1, i, half, accs[i, half])
+                copy = nc.vector.tensor_copy if half == 1 and i >= 2 else nc.scalar.copy
+                copy(staged[:, half, :], accs[i, half][:])
+                nc.sync.dma_start(out_rows[:, 2 * half : 2 * half + 2, :], staged[:, half, :].rearrange("p (k m) -> p k m", k=2))
 
-        for i in (1, 3):
-            for half in range(2):
-                accs[i, half] = bank_tile(3 + i + half)
-                out_pass(0, i * PIECE, half, accs[i, half], True, False)
-        sums = [open_sum([last - 1, last], i * PIECE, i) for i in range(4)]
-        y_put_off = held([P, M - PIECE], F32, f"d{last - 1}")
-        y_last = held([P, 2 * PIECE], F32, f"d{last}")
-        tail_rows(0)
-        tail_rows(1)
-        tail_codes(0)
-        y_end = held([P, 2 * PIECE], F32, "zt1_0")
-        tail_rows(2)
-        tail_codes(1)
-        tail_rows(3)
-        finish_out(0)
-        tail_codes(2)
-        tail_codes(3)
-        for i in range(1, 4):
-            finish_out(i)
+        for step in range(PIECES + 2):
+            if step < PIECES:
+                gather_rows(7, y_pair[step][:, 1, :], gd[7], step * PIECE, PIECE)
+            if 1 <= step <= PIECES:
+                pair_sum(step - 1)
+                weave(step - 1)
+            if step >= 2:
+                tail_codes(step - 2)
+                finish_out(step - 2)

@@ -28,6 +28,8 @@ PIECES = M // PIECE
 PER_COL = 16
 PAGES = 3
 KIB = 1024
+TAIL_PARTS = [(0, 128), (128, 256), (384, 256), (640, 256), (896, 128)]
+PUT_OFF_FROM = 2
 
 
 def tile_list_fibre_nonlinear_deinterleave_kernel(
@@ -53,7 +55,7 @@ def tile_list_fibre_nonlinear_deinterleave_kernel(
         idx2 = held([P, S // PER_COL], U16, "idx2")
         idx3 = held([P, M // PER_COL], U16, "idx3")
         tab_w = [placed([P, T], I32, f"tab_w{a}", 48 + 8 * a) for a in range(PASSES)]
-        tab_s = held([P, PASSES, T], U8, "tab_s")
+        tab_s = held([P, T], U8, "tab_s")
         v_w = [held([P, S], U32, f"v_w{a}") for a in range(PASSES)]
         v_s = [held([P, S], U8, f"v_s{a}") for a in range(PASSES)]
         w1_early = [held([P, PASSES, 2 * PIECE], U8, f"w1_early{i}") for i in range(2)]
@@ -65,8 +67,8 @@ def tile_list_fibre_nonlinear_deinterleave_kernel(
         w3_s = held([P, PASSES, N], U8, "w3_s")
         sq_w = [held([P, S], U32, f"sq_w{a}") for a in range(PASSES)]
         sq_s = [held([P, S], U8, f"sq_s{a}") for a in range(PASSES)]
-        w2_w = [held([P, PASSES, PIECE], U32, f"w2_w{i}") for i in range(2)]
-        w2_s = [held([P, PASSES, PIECE], U8, f"w2_s{i}") for i in range(2)]
+        w2_w = {i: held([P, PASSES, width], U32, f"w2_w{i}") for i, width in ((0, PIECE), (2, P), (3, P))}
+        w2_s = {i: held([P, PASSES, width], U8, f"w2_s{i}") for i, width in ((0, PIECE), (2, P), (3, P))}
         w2_w_dealt = [held([P, K_PASS], U32, f"w2_w_dealt{a}") for a in range(PASSES)]
         w2_s_dealt = [held([P, K_PASS], U8, f"w2_s_dealt{a}") for a in range(PASSES)]
         z_w = {}
@@ -82,14 +84,15 @@ def tile_list_fibre_nonlinear_deinterleave_kernel(
         d = {c: d_early[c][:] for c in range(PACK)}
         d.update({PACK + t: d_pair[t // 2][:, t % 2, :] for t in range(PACK)})
 
-        nc.gpsimd.memset(tab_s[:].rearrange("p a t -> p (a t)").bitcast(I32), 0)
+        nc.gpsimd.memset(tab_s[:].bitcast(I32), 0)
+        nc.gpsimd.memset(v_s[1][:].bitcast(I32), 0)
+        nc.gpsimd.memset(w3_s[:].rearrange("p a t -> p (a t)").bitcast(I32), 0)
         nc.vector.memset(w1_s[:].rearrange("p a t -> p (a t)").bitcast(I32), 0)
         for page in pages:
             nc.vector.memset(page[:], 0.0)
-        nc.vector.memset(w3_s[:].rearrange("p a t -> p (a t)").bitcast(I32), 0)
 
-        def load_scale_rows(plane, scales):
-            for r in range(4):
+        def load_scale_rows(plane, scales, rows=range(4)):
+            for r in rows:
                 nc.sync.dma_start(
                     plane[r:P:32, :, :].bitcast(I32),
                     scales[:, r:16:4, :].rearrange("a q n -> q a n").bitcast(I32),
@@ -109,28 +112,42 @@ def tile_list_fibre_nonlinear_deinterleave_kernel(
 
         w1_bytes = w1_words.rearrange("a p n -> p a n")
         xn_raw, w2_raw = {}, {}
-        load_scale_rows(tab_s, tab_scales)
+        for q in range(4):
+            nc.sync.dma_start(tab_s[32 * q : 32 * q + 8, :].bitcast(I32), tab_scales[:, 4 * q : 4 * q + 4, :].bitcast(I32))
         nc.sync.dma_start(idx1[:], offs)
         nc.sync.dma_start(idx2[:], offs2)
-        nc.sync.dma_start(idx3[:], offs3)
-        nc.sync.dma_start(w1_early[0][:].bitcast(I32), w1_bytes[:, :, : 2 * PIECE].bitcast(I32))
         for a in range(PASSES):
             xn_raw[a, 0] = load_rows(xn, a, 0, f"raw{a}")
         for a in range(PASSES):
             w2_raw[a, 0] = load_rows(w2, a, 0, f"raw{2 + a}")
         load_table_words(0)
         load_scale_rows(w1_s, w1_scales)
+        nc.sync.dma_start(w1_early[0][:].bitcast(I32), w1_bytes[:, :, : 2 * PIECE].bitcast(I32))
         load_table_words(1)
+        nc.vector.tensor_copy(v_s[0][:], tab_s[:].indirect(idx1[:]))
+        for first, last in ((0, 64), (64, P - 4)):
+            nc.sync.dma_start(v_s[1][first:last, :].bitcast(I32), v_s[0][first + 4 : last + 4, :].bitcast(I32))
         nc.sync.dma_start(weights[:, :PIECE], wgs[:, :PIECE])
+
+        def load_narrow(matrix, a, first, raw):
+            rows = matrix[a * K_PASS : (a + 1) * K_PASS, first : first + P]
+            nc.sync.dma_start(raw[:], rows.rearrange("(p t) w -> p t w", t=PACK))
+            return raw
+
         xn_raw[0, 1] = load_rows(xn, 0, 1, "raw4")
-        xn_raw[1, 1] = load_rows(xn, 1, 1, "xn_last1")
-        nc.sync.dma_start(weights[:, PIECE:], wgs[:, PIECE:])
-        w2_raw[0, 1] = load_rows(w2, 0, 1, "raw5")
-        w2_raw[1, 1] = load_rows(w2, 1, 1, "w2_last")
+        xn_halves = [load_narrow(xn, 1, PIECE + i * P, held([P, PACK, P], F32, f"xn_half{i}")) for i in range(2)]
+        nc.sync.dma_start(weights[:, PIECE : 2 * PIECE], wgs[:, PIECE : 2 * PIECE])
+        w2_raw[0, 2] = load_narrow(w2, 0, 2 * P, held([P, PACK, P], F32, "raw5"))
+        w2_raw[1, 2] = load_narrow(w2, 1, 2 * P, held([P, PACK, P], F32, "w2_last"))
         nc.sync.dma_start(w1_early[1][:].bitcast(I32), w1_bytes[:, :, 2 * PIECE : 4 * PIECE].bitcast(I32))
         for piece in (2, 3):
             xn_raw[0, piece] = load_rows(xn, 0, piece, f"raw{4 + piece}")
             xn_raw[1, piece] = load_rows(xn, 1, piece, f"xn_last{piece}")
+            if piece == 2:
+                nc.sync.dma_start(weights[:, 2 * PIECE :], wgs[:, 2 * PIECE :])
+        for a in range(PASSES):
+            w2_raw[a, 3] = load_narrow(w2, a, 3 * P, held([P, PACK, P], F32, "xn_half0" if a == 0 else "xn_last1"))
+        nc.sync.dma_start(idx3[:], offs3)
         with nc.allow_non_contiguous_dma(reason="one gain a partition"):
             nc.sync.dma_start(gain_early[:], gain[:K_PASS].rearrange("(c p) -> p c", p=P))
         nc.sync.dma_start(gain_dealt[:], gain[K_PASS:].rearrange("(p t) -> p t", t=PACK))
@@ -146,20 +163,20 @@ def tile_list_fibre_nonlinear_deinterleave_kernel(
             nc.sync.dma_start(w2_late[a][:], rows.rearrange("(p t) w -> p t w", t=PACK))
 
         load_w2_late(0)
-        load_weights_dealt(0)
-        load_w2_late(1)
         nc.sync.dma_start(d[1], disp[P : 2 * P, :])
+        load_w2_late(1)
+        load_weights_dealt(0)
         nc.sync.dma_start(w1_late[:].bitcast(I32), w1_bytes[:, :, 2 * K_PASS :].bitcast(I32))
         nc.sync.dma_start(d[2], disp[2 * P : 3 * P, :])
         late_rows = disp[K_PASS:, :].rearrange("(p t) m -> p t m", t=PACK)
-        load_weights_dealt(1)
         nc.sync.dma_start(d[3], disp[3 * P : 4 * P, :])
+        load_weights_dealt(1)
         nc.sync.dma_start(d_pair[0][:], late_rows[:, 0:2, :])
         load_weights_dealt(2)
         nc.sync.dma_start(d_pair[1][:], late_rows[:, 2:4, :])
-        load_weights_dealt(3)
         nc.sync.dma_start(w3_w[:], w3_words.rearrange("a p n i -> p a (n i)").bitcast(I32))
         load_scale_rows(w3_s, w3_scales)
+        load_weights_dealt(3)
 
         def interleave(grouped, raw, func):
             nc.scalar.activation(
@@ -170,23 +187,27 @@ def tile_list_fibre_nonlinear_deinterleave_kernel(
             cols = slice(piece * PIECE, (piece + 1) * PIECE)
             for a in range(PASSES):
                 grouped = ring.tile([P, PIECE, PACK], BF16, name="sq_grouped", align_bytes=64)
-                interleave(grouped[:], xn_raw[a, piece], ACT.Square)
+                if (a, piece) == (1, 1):
+                    for i in range(2):
+                        interleave(grouped[:, i * P : (i + 1) * P, :], xn_halves[i], ACT.Square)
+                else:
+                    interleave(grouped[:], xn_raw[a, piece], ACT.Square)
                 nc.vector.quantize_mx(sq_w[a][:, cols].bitcast(FP8X4), sq_s[a][:, cols], grouped[:].rearrange("p w t -> p (w t)"))
 
-        def quantise_w2(piece):
-            grouped = held([P, PASSES, PIECE, PACK], BF16, f"w2_grouped{piece}")
+        def quantise_w2(c):
+            grouped = held([P, PASSES, PIECE if c == 0 else P, PACK], BF16, {0: "w2_grouped0", 2: "w2_grouped1", 3: "turned_pair0"}[c])
             for a in range(PASSES):
-                interleave(grouped[:, a, :, :], w2_raw[a, piece], ACT.Copy)
+                interleave(grouped[:, a, :, :], w2_raw[a, c], ACT.Copy)
             nc.vector.quantize_mx(
-                w2_w[piece][:].rearrange("p a w -> p (a w)").bitcast(FP8X4),
-                w2_s[piece][:].rearrange("p a w -> p (a w)"),
+                w2_w[c][:].rearrange("p a w -> p (a w)").bitcast(FP8X4),
+                w2_s[c][:].rearrange("p a w -> p (a w)"),
                 grouped[:].rearrange("p a w t -> p (a w t)"),
             )
 
         def quantise_w2_dealt(a):
             grouped = held([P, PACK, P, PACK], BF16, f"w2_grouped{a}")
             nc.scalar.activation(
-                grouped[:].rearrange("p t m j -> p m t j"), w2_late[a][:].rearrange("p j (m t) -> p m t j", t=PACK), ACT.Copy
+                grouped[:].rearrange("p t m j -> p m j t"), w2_late[a][:].rearrange("p j (m t) -> p m j t", t=PACK), ACT.Copy
             )
             nc.vector.quantize_mx(w2_w_dealt[a][:].bitcast(FP8X4), w2_s_dealt[a][:], grouped[:].rearrange("p t m j -> p (t m j)"))
 
@@ -200,8 +221,9 @@ def tile_list_fibre_nonlinear_deinterleave_kernel(
             if c < PACK:
                 piece, first = divmod(c * P, PIECE)
                 cols = slice(first, first + P)
+                part, w2_cols = (0, cols) if piece == 0 else (c, slice(0, P))
                 return (
-                    w2_w[piece][:, a, cols], w2_s[piece][:, a, cols],
+                    w2_w[part][:, a, w2_cols], w2_s[part][:, a, w2_cols],
                     w1_early[piece][:, a, 2 * first : 2 * (first + P)], w1_s[:, a, c * P : (c + 1) * P],
                 )
             t = c - PACK
@@ -211,18 +233,14 @@ def tile_list_fibre_nonlinear_deinterleave_kernel(
         def make_h(c, first, count, number, values):
             acc = bank_tile(number)
             cols = slice(first, first + count)
+            squares, table = [], []
             for a in range(PASSES):
-                codes, scales, unused_codes, unused_scales = stationary(c, a)
-                nc.tensor.matmul_mx(
-                    acc[:, :count], codes.bitcast(FP8X4), scales,
-                    sq_w[a][:, cols].bitcast(FP8X4), sq_s[a][:, cols], start=(a == 0), stop=False,
-                )
-            for a in range(PASSES):
-                unused_codes, unused_scales, codes, scales = stationary(c, a)
-                nc.tensor.matmul_mx(
-                    acc[:, :count], codes.bitcast(FP4X4), scales,
-                    v_w[a][:, cols].bitcast(FP8X4), v_s[a][:, cols], start=False, stop=(a == PASSES - 1),
-                )
+                w2_codes, w2_scales, w1_codes, w1_scale_bytes = stationary(c, a)
+                squares.append((w2_codes.bitcast(FP8X4), w2_scales, sq_w[a][:, cols].bitcast(FP8X4), sq_s[a][:, cols]))
+                table.append((w1_codes.bitcast(FP4X4), w1_scale_bytes, v_w[a][:, cols].bitcast(FP8X4), v_s[a][:, cols]))
+            passes = squares + table if first == 0 and c < 2 else table + squares
+            for n, operands in enumerate(passes):
+                nc.tensor.matmul_mx(acc[:, :count], *operands, start=(n == 0), stop=(n == len(passes) - 1))
             nc.scalar.activation(values, acc[:, :count], ACT.Tanh)
 
         def scatter_h(c, first, count, values):
@@ -269,18 +287,18 @@ def tile_list_fibre_nonlinear_deinterleave_kernel(
             nc.vector.quantize_mx(codes[:, cols].bitcast(FP8X4), z_s[0][:, cols], words[:].rearrange("p m u -> p (m u)").bitcast(BF16))
 
         def out_pass(a, i, half, acc):
-            cols = slice(i * PIECE, (i + 1) * PIECE)
-            for k in range(2):
-                n0 = (2 * half + k) * P
+            first, count = TAIL_PARTS[i]
+            cols = slice(first, first + count)
+            tiles = BANK // count
+            for k in range(tiles):
+                n0 = (tiles * half + k) * P
                 nc.tensor.matmul_mx(
-                    acc[:, k * PIECE : (k + 1) * PIECE],
+                    acc[:, k * count : (k + 1) * count],
                     w3_w[:, a, n0 : n0 + P].bitcast(FP8X4), w3_s[:, a, n0 : n0 + P],
                     z_w[a, i].bitcast(FP8X4), z_s[a][:, cols],
-                    start=(a == 0 and k == 0), stop=(a == 1 and k == 1),
+                    start=(a == 0 and k == 0), stop=(a == 1 and k == tiles - 1),
                 )
 
-        for a in range(PASSES):
-            nc.vector.tensor_copy(v_s[a][:], tab_s[:, a, :].indirect(idx1[:]))
         ident = held([P, P], F32, "tab_s")
         make_identity(nc, ident[:])
         quantise_sq(0)
@@ -304,9 +322,9 @@ def tile_list_fibre_nonlinear_deinterleave_kernel(
         middle = {1: 50, 2: 58, 3: 34}
         h.update({c: placed([P, S], F32, f"h{c}", middle[c]) for c in (1, 2)})
         quantise_sq(1)
-        head_piece(1, 0, spent("xn_last1"))
+        head_piece(1, 0, spent("xn_half1"))
         head_piece(0, 1, piece_of(0, 1))
-        quantise_w2(1)
+        quantise_w2(2)
         head_piece(1, 1, spent("w2_last"))
         head_piece(2, 0, piece_of(2, 0))
         for piece in (2, 3):
@@ -322,9 +340,10 @@ def tile_list_fibre_nonlinear_deinterleave_kernel(
                 make_h(c, half * BANK, BANK, 6 + half, values[:, half * BANK : (half + 1) * BANK])
 
         gd = {0: gain_plus_disp(0, held([P, M], F32, "gd0"))}
-        for a in range(PASSES):
-            quantise_w2_dealt(a)
+        quantise_w2(3)
+        quantise_w2_dealt(0)
         gd[1] = gain_plus_disp(1, held([P, M], F32, "gd1"))
+        quantise_w2_dealt(1)
         make_h_tile(3, placed([P, S], F32, "h3", middle[3]))
         nc.scalar.copy(w1_dealt[:], w1_late[:].rearrange("p a (m t) -> p a t m", t=PACK))
 
@@ -354,19 +373,21 @@ def tile_list_fibre_nonlinear_deinterleave_kernel(
         codes0 = placed([P, M], U32, "codes0", middle[2] + 2)
         for half in range(2):
             quantise_z0(half, zt[half], codes0)
-        for i in range(PIECES):
-            z_w[0, i] = codes0[:, i * PIECE : (i + 1) * PIECE]
+        for i, (first, count) in enumerate(TAIL_PARTS):
+            z_w[0, i] = codes0[:, first : first + count]
         y5 = held([P, M], F32, "h0")
         gather_rows(5, y5[:], gd[5], 0, M)
         gd[6] = gain_plus_disp(6, placed([P, M], F32, "gd6", 40))
         make_h_tile(7, placed([P, S], F32, "h7", 44))
         turn_pair(1, y5[:], False, True)
-        y_pair = [held([P, 2, PIECE], F32, name) for name in ("xn_last1", "xn_last2", "xn_last3", "w2_last")]
-        for i in range(PIECES):
-            gather_rows(6, y_pair[i][:, 0, :], gd[6], i * PIECE, PIECE)
+        y_pair = {i: held([P, 2, TAIL_PARTS[i][1]], F32, f"xn_last{i + 1}") for i in range(PUT_OFF_FROM)}
+        for i in range(PUT_OFF_FROM):
+            gather_rows(6, y_pair[i][:, 0, :], gd[6], *TAIL_PARTS[i])
         scatter_h(7, 0, S, h[7][:])
+        for i, kib in zip(range(PUT_OFF_FROM, len(TAIL_PARTS)), (44, 46, 12)):
+            y_pair[i] = placed([P, 2, TAIL_PARTS[i][1]], F32, f"y_pair{i}", kib)
 
-        halves = [held([P, 2, PIECE], F32, f"d{i}") for i in range(PIECES)]
+        halves = [held([P, 2, count], F32, name) for (first, count), name in zip(TAIL_PARTS, ("d0", "d1", "d2", "d3", "gd0"))]
         turned_pair = []
         for i in range(PIECES):
             turned_pair.append(held([P, 2, P, 2], BF16, f"turned_pair{i}"))
@@ -378,52 +399,65 @@ def tile_list_fibre_nonlinear_deinterleave_kernel(
                 nc.tensor.transpose(
                     bank[:, place * P : (place + 1) * P], turned_pair[i][:, k, :, :].rearrange("m p e -> m (p e)").bitcast(F32), ident[:]
                 )
-            for i in (2 * n, 2 * n + 1):
-                nc.scalar.copy(halves[i][:, 0, :], bank[:, (i % 2) * PIECE : (i % 2 + 1) * PIECE])
+            for i, (first, count) in enumerate(TAIL_PARTS):
+                lo, hi = max(first, n * BANK), min(first + count, (n + 1) * BANK)
+                if lo < hi:
+                    nc.scalar.copy(halves[i][:, 0, lo - first : hi - first], bank[:, lo - n * BANK : hi - n * BANK])
         gd[7] = gain_plus_disp(7, held([P, M], F32, "h0"))
         accs = {}
-        for i in range(PIECES):
-            for half in range(2):
-                accs[i, half] = bank_tile((6 + 2 * i + half) % 8)
+        for i, (first, count) in enumerate(TAIL_PARTS):
+            for half in range(count // P):
+                accs[i, half] = bank_tile((6 + first // P + half) % 8)
                 out_pass(0, i, half, accs[i, half])
 
         def pair_sum(i):
+            first, count = TAIL_PARTS[i]
             nc.vector.tensor_tensor(
                 halves[i][:, 1, :].bitcast(BF16).rearrange("p (m e) -> p m e", e=2),
                 y_pair[i][:].rearrange("p e m -> p m e"),
-                d_pair[1][:, :, i * PIECE : (i + 1) * PIECE].rearrange("p e m -> p m e"),
+                d_pair[1][:, :, first : first + count].rearrange("p e m -> p m e"),
                 ADD,
             )
 
-        woven = [held([P, PIECE, 2], F32, f"raw{4 + i}") for i in range(PIECES)]
+        woven = [held([P, count, 2], F32, name) for (first, count), name in zip(TAIL_PARTS, ("raw4", "raw5", "raw6", "raw7", "gd1"))]
 
         def weave(i):
-            copy = nc.scalar.copy if i < 2 else nc.vector.tensor_copy
+            copy = nc.scalar.copy if i < 3 else nc.vector.tensor_copy
             copy(woven[i][:], halves[i][:].rearrange("p u m -> p m u"))
 
         def tail_codes(i):
-            words = woven[i]
-            codes = held([P, PIECE], U32, f"z_w1_{i}")
+            first, count = TAIL_PARTS[i]
+            codes = held([P, count], U32, f"z_w1_{i}")
             z_w[1, i] = codes[:]
             nc.vector.quantize_mx(
-                codes[:].bitcast(FP8X4), z_s[1][:, i * PIECE : (i + 1) * PIECE], words[:].rearrange("p m u -> p (m u)").bitcast(BF16)
+                codes[:].bitcast(FP8X4), z_s[1][:, first : first + count], woven[i][:].rearrange("p m u -> p (m u)").bitcast(BF16)
             )
 
-        def finish_out(i):
-            staged = placed([P, 2, BANK], F32, f"staged{i}", 16 + 4 * i)
-            out_rows = out[:, i * PIECE : (i + 1) * PIECE].rearrange("(k p) m -> p k m", p=P)
-            for half in range(2):
-                out_pass(1, i, half, accs[i, half])
-                copy = nc.vector.tensor_copy if half == 1 and i >= 2 else nc.scalar.copy
-                copy(staged[:, half, :], accs[i, half][:])
-                nc.sync.dma_start(out_rows[:, 2 * half : 2 * half + 2, :], staged[:, half, :].rearrange("p (k m) -> p k m", k=2))
+        def finish_out(i, half):
+            first, count = TAIL_PARTS[i]
+            tiles = BANK // count
+            staged = placed([P, BANK], F32, f"staged{i}_{half}", 16 + 2 * (first // P + half))
+            out_rows = out[:, first : first + count].rearrange("(k p) m -> p k m", p=P)
+            out_pass(1, i, half, accs[i, half])
+            copy = nc.vector.tensor_copy if (i, half) == (3, 1) else nc.scalar.copy
+            copy(staged[:], accs[i, half][:])
+            nc.sync.dma_start(out_rows[:, tiles * half : tiles * (half + 1), :], staged[:].rearrange("p (k m) -> p k m", k=tiles))
 
-        for step in range(PIECES + 2):
-            if step < PIECES:
-                gather_rows(7, y_pair[step][:, 1, :], gd[7], step * PIECE, PIECE)
-            if 1 <= step <= PIECES:
-                pair_sum(step - 1)
-                weave(step - 1)
-            if step >= 2:
-                tail_codes(step - 2)
-                finish_out(step - 2)
+        def sum_and_weave(i):
+            if i >= PUT_OFF_FROM:
+                for c in (7, 6):
+                    gather_rows(c, y_pair[i][:, c - 6, :], gd[c], *TAIL_PARTS[i])
+            pair_sum(i)
+            weave(i)
+
+        for i in range(PUT_OFF_FROM):
+            gather_rows(7, y_pair[i][:, 1, :], gd[7], *TAIL_PARTS[i])
+        sum_and_weave(0)
+        for i, (first, count) in enumerate(TAIL_PARTS):
+            if i < 1:
+                sum_and_weave(i + 1)
+            tail_codes(i)
+            finish_out(i, 0)
+            if 1 <= i < len(TAIL_PARTS) - 1:
+                sum_and_weave(i + 1)
+                finish_out(i, 1)

@@ -387,7 +387,7 @@ def tile_list_fibre_nonlinear_deinterleave_kernel(
         for i, kib in zip(range(PUT_OFF_FROM, len(TAIL_PARTS)), (44, 46, 12)):
             y_pair[i] = placed([P, 2, TAIL_PARTS[i][1]], F32, f"y_pair{i}", kib)
 
-        halves = [held([P, 2, count], F32, name) for (first, count), name in zip(TAIL_PARTS, ("d0", "d1", "d2", "d3", "gd0"))]
+        woven = [held([P, count, 2], F32, name) for (first, count), name in zip(TAIL_PARTS, ("d0", "d1", "d2", "d3", "gd0"))]
         turned_pair = []
         for i in range(PIECES):
             turned_pair.append(held([P, 2, P, 2], BF16, f"turned_pair{i}"))
@@ -402,7 +402,7 @@ def tile_list_fibre_nonlinear_deinterleave_kernel(
             for i, (first, count) in enumerate(TAIL_PARTS):
                 lo, hi = max(first, n * BANK), min(first + count, (n + 1) * BANK)
                 if lo < hi:
-                    nc.scalar.copy(halves[i][:, 0, lo - first : hi - first], bank[:, lo - n * BANK : hi - n * BANK])
+                    nc.scalar.copy(woven[i][:, lo - first : hi - first, 0], bank[:, lo - n * BANK : hi - n * BANK])
         gd[7] = gain_plus_disp(7, held([P, M], F32, "h0"))
         accs = {}
         for i, (first, count) in enumerate(TAIL_PARTS):
@@ -413,17 +413,11 @@ def tile_list_fibre_nonlinear_deinterleave_kernel(
         def pair_sum(i):
             first, count = TAIL_PARTS[i]
             nc.vector.tensor_tensor(
-                halves[i][:, 1, :].bitcast(BF16).rearrange("p (m e) -> p m e", e=2),
+                woven[i][:].bitcast(BF16)[:, :, 2:4],
                 y_pair[i][:].rearrange("p e m -> p m e"),
                 d_pair[1][:, :, first : first + count].rearrange("p e m -> p m e"),
                 ADD,
             )
-
-        woven = [held([P, count, 2], F32, name) for (first, count), name in zip(TAIL_PARTS, ("raw4", "raw5", "raw6", "raw7", "gd1"))]
-
-        def weave(i):
-            copy = nc.scalar.copy if i < 3 else nc.vector.tensor_copy
-            copy(woven[i][:], halves[i][:].rearrange("p u m -> p m u"))
 
         def tail_codes(i):
             first, count = TAIL_PARTS[i]
@@ -448,7 +442,6 @@ def tile_list_fibre_nonlinear_deinterleave_kernel(
                 for c in (7, 6):
                     gather_rows(c, y_pair[i][:, c - 6, :], gd[c], *TAIL_PARTS[i])
             pair_sum(i)
-            weave(i)
 
         for i in range(PUT_OFF_FROM):
             gather_rows(7, y_pair[i][:, 1, :], gd[7], *TAIL_PARTS[i])

@@ -413,9 +413,9 @@ def tile_list_fibre_nonlinear_deinterleave_kernel(
         def pair_sum(i):
             first, count = TAIL_PARTS[i]
             nc.vector.tensor_tensor(
-                woven[i][:].bitcast(BF16)[:, :, 2:4],
-                y_pair[i][:].rearrange("p e m -> p m e"),
-                d_pair[1][:, :, first : first + count].rearrange("p e m -> p m e"),
+                woven[i][:].bitcast(BF16)[:, :, 2:4].rearrange("p (c i) e -> p c e i", i=4),
+                y_pair[i][:].rearrange("p e (c i) -> p c e i", i=4),
+                d_pair[1][:, :, first : first + count].rearrange("p e (c i) -> p c e i", i=4),
                 ADD,
             )
 

@@ -122,12 +122,11 @@ def tile_list_fibre_nonlinear_deinterleave_kernel(
             w2_raw[a, 0] = load_rows(w2, a, 0, f"raw{2 + a}")
         load_table_words(0)
         load_scale_rows(w1_s, w1_scales)
-        nc.sync.dma_start(w1_early[0][:].bitcast(I32), w1_bytes[:, :, : 2 * PIECE].bitcast(I32))
         load_table_words(1)
+        nc.sync.dma_start(w1_early[0][:].bitcast(I32), w1_bytes[:, :, : 2 * PIECE].bitcast(I32))
         nc.vector.tensor_copy(v_s[0][:], tab_s[:].indirect(idx1[:]))
-        for first, last in ((0, 64), (64, P - 4)):
-            nc.sync.dma_start(v_s[1][first:last, :].bitcast(I32), v_s[0][first + 4 : last + 4, :].bitcast(I32))
-        nc.sync.dma_start(weights[:, :PIECE], wgs[:, :PIECE])
+        for r in range(4):
+            nc.sync.dma_start(v_s[1][r:P:32, :].bitcast(I32), v_s[0][4 + r : P : 32, :].bitcast(I32))
 
         def load_narrow(matrix, a, first, raw):
             rows = matrix[a * K_PASS : (a + 1) * K_PASS, first : first + P]
@@ -135,6 +134,7 @@ def tile_list_fibre_nonlinear_deinterleave_kernel(
             return raw
 
         xn_raw[0, 1] = load_rows(xn, 0, 1, "raw4")
+        nc.sync.dma_start(weights[:, :PIECE], wgs[:, :PIECE])
         xn_halves = [load_narrow(xn, 1, PIECE + i * P, held([P, PACK, P], F32, f"xn_half{i}")) for i in range(2)]
         nc.sync.dma_start(weights[:, PIECE : 2 * PIECE], wgs[:, PIECE : 2 * PIECE])
         w2_raw[0, 2] = load_narrow(w2, 0, 2 * P, held([P, PACK, P], F32, "raw5"))
@@ -379,13 +379,12 @@ def tile_list_fibre_nonlinear_deinterleave_kernel(
         gather_rows(5, y5[:], gd[5], 0, M)
         gd[6] = gain_plus_disp(6, placed([P, M], F32, "gd6", 40))
         make_h_tile(7, placed([P, S], F32, "h7", 44))
+        gd[7] = gain_plus_disp(7, held([P, M], F32, "gd1"))
         turn_pair(1, y5[:], False, True)
         y_pair = {i: held([P, 2, TAIL_PARTS[i][1]], F32, f"xn_last{i + 1}") for i in range(PUT_OFF_FROM)}
         for i in range(PUT_OFF_FROM):
             gather_rows(6, y_pair[i][:, 0, :], gd[6], *TAIL_PARTS[i])
         scatter_h(7, 0, S, h[7][:])
-        for i, kib in zip(range(PUT_OFF_FROM, len(TAIL_PARTS)), (44, 46, 12)):
-            y_pair[i] = placed([P, 2, TAIL_PARTS[i][1]], F32, f"y_pair{i}", kib)
 
         woven = [held([P, count, 2], F32, name) for (first, count), name in zip(TAIL_PARTS, ("d0", "d1", "d2", "d3", "gd0"))]
         turned_pair = []
@@ -403,7 +402,6 @@ def tile_list_fibre_nonlinear_deinterleave_kernel(
                 lo, hi = max(first, n * BANK), min(first + count, (n + 1) * BANK)
                 if lo < hi:
                     nc.scalar.copy(woven[i][:, lo - first : hi - first, 0], bank[:, lo - n * BANK : hi - n * BANK])
-        gd[7] = gain_plus_disp(7, held([P, M], F32, "h0"))
         accs = {}
         for i, (first, count) in enumerate(TAIL_PARTS):
             for half in range(count // P):
@@ -439,6 +437,7 @@ def tile_list_fibre_nonlinear_deinterleave_kernel(
 
         def sum_and_weave(i):
             if i >= PUT_OFF_FROM:
+                y_pair[i] = held([P, 2, TAIL_PARTS[i][1]], F32, f"xn_last{i % 2 + 1}")
                 for c in (7, 6):
                     gather_rows(c, y_pair[i][:, c - 6, :], gd[c], *TAIL_PARTS[i])
             pair_sum(i)

@@ -120,9 +120,9 @@ def tile_list_fibre_nonlinear_deinterleave_kernel(
             xn_raw[a, 0] = load_rows(xn, a, 0, f"raw{a}")
         for a in range(PASSES):
             w2_raw[a, 0] = load_rows(w2, a, 0, f"raw{2 + a}")
-        load_table_words(0)
-        load_scale_rows(w1_s, w1_scales)
-        load_table_words(1)
+            load_scale_rows(w1_s, w1_scales, (2 * a, 2 * a + 1))
+        for a in range(PASSES):
+            load_table_words(a)
         nc.sync.dma_start(w1_early[0][:].bitcast(I32), w1_bytes[:, :, : 2 * PIECE].bitcast(I32))
         nc.vector.tensor_copy(v_s[0][:], tab_s[:].indirect(idx1[:]))
         for r in range(4):
@@ -133,13 +133,13 @@ def tile_list_fibre_nonlinear_deinterleave_kernel(
             nc.sync.dma_start(raw[:], rows.rearrange("(p t) w -> p t w", t=PACK))
             return raw
 
-        xn_raw[0, 1] = load_rows(xn, 0, 1, "raw4")
-        nc.sync.dma_start(weights[:, :PIECE], wgs[:, :PIECE])
-        xn_halves = [load_narrow(xn, 1, PIECE + i * P, held([P, PACK, P], F32, f"xn_half{i}")) for i in range(2)]
-        nc.sync.dma_start(weights[:, PIECE : 2 * PIECE], wgs[:, PIECE : 2 * PIECE])
         w2_raw[0, 2] = load_narrow(w2, 0, 2 * P, held([P, PACK, P], F32, "raw5"))
+        nc.sync.dma_start(weights[:, :PIECE], wgs[:, :PIECE])
         w2_raw[1, 2] = load_narrow(w2, 1, 2 * P, held([P, PACK, P], F32, "w2_last"))
         nc.sync.dma_start(w1_early[1][:].bitcast(I32), w1_bytes[:, :, 2 * PIECE : 4 * PIECE].bitcast(I32))
+        xn_raw[0, 1] = load_rows(xn, 0, 1, "raw4")
+        xn_halves = [load_narrow(xn, 1, PIECE + i * P, held([P, PACK, P], F32, f"xn_half{i}")) for i in range(2)]
+        nc.sync.dma_start(weights[:, PIECE : 2 * PIECE], wgs[:, PIECE : 2 * PIECE])
         for piece in (2, 3):
             xn_raw[0, piece] = load_rows(xn, 0, piece, f"raw{4 + piece}")
             xn_raw[1, piece] = load_rows(xn, 1, piece, f"xn_last{piece}")
@@ -303,8 +303,8 @@ def tile_list_fibre_nonlinear_deinterleave_kernel(
         make_identity(nc, ident[:])
         quantise_sq(0)
         quantise_w2(0)
-        gather_words(0, 0, S)
         nc.vector.tensor_copy(w1_s_dealt[:], w1_s[:, :, K_PASS:].rearrange("p a (m t) -> p a t m", t=PACK))
+        gather_words(0, 0, S)
         gather_words(1, 0, PIECE)
 
         def head_piece(c, piece, values):
@@ -321,15 +321,11 @@ def tile_list_fibre_nonlinear_deinterleave_kernel(
         gather_words(1, PIECE, S - PIECE)
         middle = {1: 50, 2: 58, 3: 34}
         h.update({c: placed([P, S], F32, f"h{c}", middle[c]) for c in (1, 2)})
-        quantise_sq(1)
-        head_piece(1, 0, spent("xn_half1"))
-        head_piece(0, 1, piece_of(0, 1))
         quantise_w2(2)
-        head_piece(1, 1, spent("w2_last"))
-        head_piece(2, 0, piece_of(2, 0))
-        for piece in (2, 3):
+        head_piece(1, 0, spent("w2_last"))
+        for piece in (1, 2, 3):
             quantise_sq(piece)
-            head_piece(2, piece - 1, spent(f"xn_last{piece}"))
+            head_piece(2, piece - 1, spent("xn_half1" if piece == 1 else f"xn_last{piece}"))
             for c in range(2):
                 head_piece(c, piece, piece_of(c, piece))
         head_piece(2, 3, piece_of(2, 3))

@@ -134,11 +134,11 @@ def tile_list_fibre_nonlinear_deinterleave_kernel(
             return raw
 
         w2_raw[0, 2] = load_narrow(w2, 0, 2 * P, held([P, PACK, P], F32, "raw5"))
-        nc.sync.dma_start(weights[:, :PIECE], wgs[:, :PIECE])
         w2_raw[1, 2] = load_narrow(w2, 1, 2 * P, held([P, PACK, P], F32, "w2_last"))
+        nc.sync.dma_start(weights[:, :PIECE], wgs[:, :PIECE])
         nc.sync.dma_start(w1_early[1][:].bitcast(I32), w1_bytes[:, :, 2 * PIECE : 4 * PIECE].bitcast(I32))
         xn_raw[0, 1] = load_rows(xn, 0, 1, "raw4")
-        xn_halves = [load_narrow(xn, 1, PIECE + i * P, held([P, PACK, P], F32, f"xn_half{i}")) for i in range(2)]
+        xn_raw[1, 1] = load_rows(xn, 1, 1, "xn_last1")
         nc.sync.dma_start(weights[:, PIECE : 2 * PIECE], wgs[:, PIECE : 2 * PIECE])
         for piece in (2, 3):
             xn_raw[0, piece] = load_rows(xn, 0, piece, f"raw{4 + piece}")
@@ -146,7 +146,7 @@ def tile_list_fibre_nonlinear_deinterleave_kernel(
             if piece == 2:
                 nc.sync.dma_start(weights[:, 2 * PIECE :], wgs[:, 2 * PIECE :])
         for a in range(PASSES):
-            w2_raw[a, 3] = load_narrow(w2, a, 3 * P, held([P, PACK, P], F32, "xn_half0" if a == 0 else "xn_last1"))
+            w2_raw[a, 3] = load_narrow(w2, a, 3 * P, held([P, PACK, P], F32, f"w2_tile3_{a}"))
         nc.sync.dma_start(idx3[:], offs3)
         with nc.allow_non_contiguous_dma(reason="one gain a partition"):
             nc.sync.dma_start(gain_early[:], gain[:K_PASS].rearrange("(c p) -> p c", p=P))
@@ -187,11 +187,7 @@ def tile_list_fibre_nonlinear_deinterleave_kernel(
             cols = slice(piece * PIECE, (piece + 1) * PIECE)
             for a in range(PASSES):
                 grouped = ring.tile([P, PIECE, PACK], BF16, name="sq_grouped", align_bytes=64)
-                if (a, piece) == (1, 1):
-                    for i in range(2):
-                        interleave(grouped[:, i * P : (i + 1) * P, :], xn_halves[i], ACT.Square)
-                else:
-                    interleave(grouped[:], xn_raw[a, piece], ACT.Square)
+                interleave(grouped[:], xn_raw[a, piece], ACT.Square)
                 nc.vector.quantize_mx(sq_w[a][:, cols].bitcast(FP8X4), sq_s[a][:, cols], grouped[:].rearrange("p w t -> p (w t)"))
 
         def quantise_w2(c):
@@ -325,7 +321,7 @@ def tile_list_fibre_nonlinear_deinterleave_kernel(
         head_piece(1, 0, spent("w2_last"))
         for piece in (1, 2, 3):
             quantise_sq(piece)
-            head_piece(2, piece - 1, spent("xn_half1" if piece == 1 else f"xn_last{piece}"))
+            head_piece(2, piece - 1, spent(f"xn_last{piece}"))
             for c in range(2):
                 head_piece(c, piece, piece_of(c, piece))
         head_piece(2, 3, piece_of(2, 3))

@@ -107,7 +107,8 @@ def tile_list_fibre_nonlinear_deinterleave_kernel(
             else:
                 raw = held([P, PACK, PIECE], F32, name)
             rows = matrix[a * K_PASS : (a + 1) * K_PASS, piece * PIECE : (piece + 1) * PIECE]
-            nc.sync.dma_start(raw[:], rows.rearrange("(p t) w -> p t w", t=PACK))
+            queue = nc.scalar if name == "raw2" else nc.sync
+            queue.dma_start(raw[:], rows.rearrange("(p t) w -> p t w", t=PACK))
             return raw
 
         w1_bytes = w1_words.rearrange("a p n -> p a n")

@@ -58,7 +58,7 @@ def tile_list_fibre_nonlinear_deinterleave_kernel(
         tab_s = held([P, T], U8, "tab_s")
         v_w = [held([P, S], U32, f"v_w{a}") for a in range(PASSES)]
         v_s = [held([P, S], U8, f"v_s{a}") for a in range(PASSES)]
-        w1_early = [held([P, PASSES, 2 * PIECE], U8, f"w1_early{i}") for i in range(2)]
+        w1_early = held([P, PASSES, 2 * K_PASS], U8, "w1_early")
         w1_late = held([P, PASSES, K_PASS], U16, "w1_late")
         w1_dealt = held([P, PASSES, PACK, P], U16, "w1_dealt")
         w1_s = held([P, PASSES, H], U8, "w1_s")
@@ -124,10 +124,10 @@ def tile_list_fibre_nonlinear_deinterleave_kernel(
             load_scale_rows(w1_s, w1_scales, (2 * a, 2 * a + 1))
         for a in range(PASSES):
             load_table_words(a)
-        nc.sync.dma_start(w1_early[0][:].bitcast(I32), w1_bytes[:, :, : 2 * PIECE].bitcast(I32))
         nc.vector.tensor_copy(v_s[0][:], tab_s[:].indirect(idx1[:]))
         for r in range(4):
             nc.sync.dma_start(v_s[1][r:P:32, :].bitcast(I32), v_s[0][4 + r : P : 32, :].bitcast(I32))
+        nc.sync.dma_start(w1_early[:].bitcast(I32), w1_bytes[:, :, : 2 * K_PASS].bitcast(I32))
 
         def load_narrow(matrix, a, first, raw):
             rows = matrix[a * K_PASS : (a + 1) * K_PASS, first : first + P]
@@ -137,7 +137,6 @@ def tile_list_fibre_nonlinear_deinterleave_kernel(
         w2_raw[0, 2] = load_narrow(w2, 0, 2 * P, held([P, PACK, P], F32, "raw5"))
         w2_raw[1, 2] = load_narrow(w2, 1, 2 * P, held([P, PACK, P], F32, "w2_last"))
         nc.sync.dma_start(weights[:, :PIECE], wgs[:, :PIECE])
-        nc.sync.dma_start(w1_early[1][:].bitcast(I32), w1_bytes[:, :, 2 * PIECE : 4 * PIECE].bitcast(I32))
         xn_raw[0, 1] = load_rows(xn, 0, 1, "raw4")
         xn_raw[1, 1] = load_rows(xn, 1, 1, "xn_last1")
         nc.sync.dma_start(weights[:, PIECE : 2 * PIECE], wgs[:, PIECE : 2 * PIECE])
@@ -221,7 +220,7 @@ def tile_list_fibre_nonlinear_deinterleave_kernel(
                 part, w2_cols = (0, cols) if piece == 0 else (c, slice(0, P))
                 return (
                     w2_w[part][:, a, w2_cols], w2_s[part][:, a, w2_cols],
-                    w1_early[piece][:, a, 2 * first : 2 * (first + P)], w1_s[:, a, c * P : (c + 1) * P],
+                    w1_early[:, a, 2 * c * P : 2 * (c + 1) * P], w1_s[:, a, c * P : (c + 1) * P],
                 )
             t = c - PACK
             cols = slice(t * P, (t + 1) * P)

@@ -113,8 +113,8 @@ def tile_list_fibre_nonlinear_deinterleave_kernel(
 
         w1_bytes = w1_words.rearrange("a p n -> p a n")
         xn_raw, w2_raw = {}, {}
-        for q in range(4):
-            nc.sync.dma_start(tab_s[32 * q : 32 * q + 8, :].bitcast(I32), tab_scales[:, 4 * q : 4 * q + 4, :].bitcast(I32))
+        for r in range(4):
+            nc.sync.dma_start(tab_s[r:P:16, :].bitcast(I32), tab_scales[:, r:16:4, :].rearrange("a q n -> q a n").bitcast(I32))
         nc.sync.dma_start(idx1[:], offs)
         nc.sync.dma_start(idx2[:], offs2)
         for a in range(PASSES):
@@ -126,7 +126,7 @@ def tile_list_fibre_nonlinear_deinterleave_kernel(
             load_table_words(a)
         nc.vector.tensor_copy(v_s[0][:], tab_s[:].indirect(idx1[:]))
         for r in range(4):
-            nc.sync.dma_start(v_s[1][r:P:32, :].bitcast(I32), v_s[0][4 + r : P : 32, :].bitcast(I32))
+            nc.sync.dma_start(v_s[1][r:P:32, :].bitcast(I32), v_s[0][16 + r : P : 32, :].bitcast(I32))
         nc.sync.dma_start(w1_early[:].bitcast(I32), w1_bytes[:, :, : 2 * K_PASS].bitcast(I32))
 
         def load_narrow(matrix, a, first, raw):

from contextlib import ExitStack

import concourse.mybir as mybir
from concourse.masks import make_identity

K, H, N, T, S, T2, M = 1024, 1024, 512, 2048, 1024, 2048, 1024
FLOPS = 2 * (2 * K * H * S + H * N * M)

F32 = mybir.dt.float32
BF16 = mybir.dt.bfloat16
I32 = mybir.dt.int32
U32 = mybir.dt.uint32
U16 = mybir.dt.uint16
U8 = mybir.dt.uint8
FP8X4 = mybir.dt.float8_e4m3fn_x4
FP4X4 = mybir.dt.float4_e2m1fn_x4
ACT = mybir.ActivationFunctionType
MULT = mybir.AluOpType.mult
ADD = mybir.AluOpType.add

P = 128
PACK = 4
K_PASS = P * PACK
PASSES = K // K_PASS
BANK = 512
PIECE = 256
PIECES = M // PIECE
PER_COL = 16
PAGES = 3
KIB = 1024
TAIL_PARTS = [(0, 128), (128, 256), (384, 256), (640, 256), (896, 128)]
PUT_OFF_FROM = 2


def tile_list_fibre_nonlinear_deinterleave_kernel(
    tc, tab_words, tab_scales, offs, w1_words, w1_scales, xn, w2, wgs, offs2, offs3, gain, disp, w3_words, w3_scales, out
):
    nc = tc.nc
    with ExitStack() as ctx:
        keep = ctx.enter_context(tc.tile_pool(name="keep", bufs=1))
        ring = ctx.enter_context(tc.tile_pool(name="ring", bufs=3))
        laid = ctx.enter_context(tc.tile_pool(name="laid", bufs=1))
        psum = ctx.enter_context(tc.psum_pool(name="psum", bufs=1))

        def bank_tile(number):
            return psum.tile([P, BANK], F32, name=f"bank{number}")

        def held(shape, dtype, name):
            return keep.tile(shape, dtype, name=name, align_bytes=64)

        def placed(shape, dtype, name, kib):
            return laid.tile(shape, dtype, name=name, align_bytes=64, offset=kib * KIB)

        idx1 = held([P, S // PER_COL], U16, "idx1")
        idx2 = held([P, S // PER_COL], U16, "idx2")
        idx3 = held([P, M // PER_COL], U16, "idx3")
        tab_w = [placed([P, T], I32, f"tab_w{a}", 48 + 8 * a) for a in range(PASSES)]
        tab_s = held([P, T], U8, "tab_s")
        v_w = [held([P, S], U32, f"v_w{a}") for a in range(PASSES)]
        v_s = [held([P, S], U8, f"v_s{a}") for a in range(PASSES)]
        w1_early = held([P, PASSES, 2 * K_PASS], U8, "w1_early")
        w1_late = held([P, PASSES, K_PASS], U16, "w1_late")
        w1_dealt = held([P, PASSES, PACK, P], U16, "w1_dealt")
        w1_s = held([P, PASSES, H], U8, "w1_s")
        w1_s_dealt = held([P, PASSES, PACK, P], U8, "w1_s_dealt")
        w3_w = held([P, PASSES, N], I32, "w3_w")
        w3_s = held([P, PASSES, N], U8, "w3_s")
        sq_w = [held([P, S], U32, f"sq_w{a}") for a in range(PASSES)]
        sq_s = [held([P, S], U8, f"sq_s{a}") for a in range(PASSES)]
        w2_w = {i: held([P, PASSES, width], U32, f"w2_w{i}") for i, width in ((0, PIECE), (2, P), (3, P))}
        w2_s = {i: held([P, PASSES, width], U8, f"w2_s{i}") for i, width in ((0, PIECE), (2, P), (3, P))}
        w2_w_dealt = [held([P, K_PASS], U32, f"w2_w_dealt{a}") for a in range(PASSES)]
        w2_s_dealt = [held([P, K_PASS], U8, f"w2_s_dealt{a}") for a in range(PASSES)]
        z_w = {}
        z_s = [held([P, M], U8, f"z_s{a}") for a in range(PASSES)]
        weights = held([P, S], F32, "weights")
        pages = [held([P, T2], F32, f"page{i}") for i in range(PAGES)]
        gain_early = held([P, PACK], F32, "gain_early")
        gain_dealt = held([P, PACK], F32, "gain_dealt")
        h = {0: held([P, S], F32, "h0")}
        d_early = [held([P, M], F32, f"d{c}") for c in range(PACK)]
        d_pair = [placed([P, 2, M], F32, "d45", 40), held([P, 2, M], F32, "d67")]
        w2_late = [placed([P, PACK, K_PASS], F32, f"w2_late{a}", 19 + 8 * a) for a in range(PASSES)]
        d = {c: d_early[c][:] for c in range(PACK)}
        d.update({PACK + t: d_pair[t // 2][:, t % 2, :] for t in range(PACK)})

        nc.gpsimd.memset(tab_s[:].bitcast(I32), 0)
        nc.gpsimd.memset(v_s[1][:].bitcast(I32), 0)
        nc.gpsimd.memset(w3_s[:].rearrange("p a t -> p (a t)").bitcast(I32), 0)
        nc.vector.memset(w1_s[:].rearrange("p a t -> p (a t)").bitcast(I32), 0)
        for page in pages:
            nc.vector.memset(page[:], 0.0)

        def load_scale_rows(plane, scales, rows=range(4)):
            for r in rows:
                nc.sync.dma_start(
                    plane[r:P:32, :, :].bitcast(I32),
                    scales[:, r:16:4, :].rearrange("a q n -> q a n").bitcast(I32),
                )

        def load_table_words(a):
            nc.sync.dma_start(tab_w[a][:], tab_words[a].rearrange("p t i -> p (t i)").bitcast(I32))

        def load_rows(matrix, a, piece, name):
            if piece == 0:
                raw = placed([P, PACK, PIECE], F32, name, 4 * a + (0 if matrix is xn else 8))
            else:
                raw = held([P, PACK, PIECE], F32, name)
            rows = matrix[a * K_PASS : (a + 1) * K_PASS, piece * PIECE : (piece + 1) * PIECE]
            queue = nc.scalar if name == "raw2" else nc.sync
            queue.dma_start(raw[:], rows.rearrange("(p t) w -> p t w", t=PACK))
            return raw

        w1_bytes = w1_words.rearrange("a p n -> p a n")
        xn_raw, w2_raw = {}, {}
        for r in range(4):
            nc.sync.dma_start(tab_s[r:P:16, :].bitcast(I32), tab_scales[:, r:16:4, :].rearrange("a q n -> q a n").bitcast(I32))
        nc.sync.dma_start(idx1[:], offs)
        nc.sync.dma_start(idx2[:], offs2)
        for a in range(PASSES):
            xn_raw[a, 0] = load_rows(xn, a, 0, f"raw{a}")
        for a in range(PASSES):
            w2_raw[a, 0] = load_rows(w2, a, 0, f"raw{2 + a}")
            load_scale_rows(w1_s, w1_scales, (2 * a, 2 * a + 1))
        for a in range(PASSES):
            load_table_words(a)
        nc.vector.tensor_copy(v_s[0][:], tab_s[:].indirect(idx1[:]))
        for r in range(4):
            nc.sync.dma_start(v_s[1][r:P:32, :].bitcast(I32), v_s[0][16 + r : P : 32, :].bitcast(I32))
        nc.sync.dma_start(w1_early[:].bitcast(I32), w1_bytes[:, :, : 2 * K_PASS].bitcast(I32))

        def load_narrow(matrix, a, first, raw):
            rows = matrix[a * K_PASS : (a + 1) * K_PASS, first : first + P]
            nc.sync.dma_start(raw[:], rows.rearrange("(p t) w -> p t w", t=PACK))
            return raw

        w2_raw[0, 2] = load_narrow(w2, 0, 2 * P, held([P, PACK, P], F32, "raw5"))
        w2_raw[1, 2] = load_narrow(w2, 1, 2 * P, held([P, PACK, P], F32, "w2_last"))
        nc.sync.dma_start(weights[:, :PIECE], wgs[:, :PIECE])
        xn_raw[0, 1] = load_rows(xn, 0, 1, "raw4")
        xn_raw[1, 1] = load_rows(xn, 1, 1, "xn_last1")
        nc.sync.dma_start(weights[:, PIECE : 2 * PIECE], wgs[:, PIECE : 2 * PIECE])
        for piece in (2, 3):
            xn_raw[0, piece] = load_rows(xn, 0, piece, f"raw{4 + piece}")
            xn_raw[1, piece] = load_rows(xn, 1, piece, f"xn_last{piece}")
            if piece == 2:
                nc.sync.dma_start(weights[:, 2 * PIECE :], wgs[:, 2 * PIECE :])
        for a in range(PASSES):
            w2_raw[a, 3] = load_narrow(w2, a, 3 * P, held([P, PACK, P], F32, f"w2_tile3_{a}"))
        nc.sync.dma_start(idx3[:], offs3)
        with nc.allow_non_contiguous_dma(reason="one gain a partition"):
            nc.sync.dma_start(gain_early[:], gain[:K_PASS].rearrange("(c p) -> p c", p=P))
        nc.sync.dma_start(gain_dealt[:], gain[K_PASS:].rearrange("(p t) -> p t", t=PACK))
        nc.sync.dma_start(d[0], disp[:P, :])
        weights_dealt = [placed([P, S], F32, f"weights_dealt{t}", 4 * t) for t in range(PACK)]

        def load_weights_dealt(t):
            for q in range(4):
                nc.sync.dma_start(weights_dealt[t][32 * q : 32 * (q + 1), :], wgs[t:P:PACK, :])

        def load_w2_late(a):
            rows = w2[a * K_PASS : (a + 1) * K_PASS, K_PASS:]
            nc.sync.dma_start(w2_late[a][:], rows.rearrange("(p t) w -> p t w", t=PACK))

        load_w2_late(0)
        nc.sync.dma_start(d[1], disp[P : 2 * P, :])
        load_w2_late(1)
        load_weights_dealt(0)
        nc.sync.dma_start(w1_late[:].bitcast(I32), w1_bytes[:, :, 2 * K_PASS :].bitcast(I32))
        nc.sync.dma_start(d[2], disp[2 * P : 3 * P, :])
        late_rows = disp[K_PASS:, :].rearrange("(p t) m -> p t m", t=PACK)
        nc.sync.dma_start(d[3], disp[3 * P : 4 * P, :])
        load_weights_dealt(1)
        nc.sync.dma_start(d_pair[0][:], late_rows[:, 0:2, :])
        load_weights_dealt(2)
        nc.sync.dma_start(d_pair[1][:], late_rows[:, 2:4, :])
        nc.sync.dma_start(w3_w[:], w3_words.rearrange("a p n i -> p a (n i)").bitcast(I32))
        load_scale_rows(w3_s, w3_scales)
        load_weights_dealt(3)

        def interleave(grouped, raw, func):
            nc.scalar.activation(
                grouped.rearrange("p (c i) t -> p c t i", i=4), raw[:].rearrange("p t (c i) -> p c t i", i=4), func
            )

        def quantise_sq(piece):
            cols = slice(piece * PIECE, (piece + 1) * PIECE)
            for a in range(PASSES):
                grouped = ring.tile([P, PIECE, PACK], BF16, name="sq_grouped", align_bytes=64)
                interleave(grouped[:], xn_raw[a, piece], ACT.Square)
                nc.vector.quantize_mx(sq_w[a][:, cols].bitcast(FP8X4), sq_s[a][:, cols], grouped[:].rearrange("p w t -> p (w t)"))

        def quantise_w2(c):
            grouped = held([P, PASSES, PIECE if c == 0 else P, PACK], BF16, {0: "w2_grouped0", 2: "w2_grouped1", 3: "turned_pair0"}[c])
            for a in range(PASSES):
                interleave(grouped[:, a, :, :], w2_raw[a, c], ACT.Copy)
            nc.vector.quantize_mx(
                w2_w[c][:].rearrange("p a w -> p (a w)").bitcast(FP8X4),
                w2_s[c][:].rearrange("p a w -> p (a w)"),
                grouped[:].rearrange("p a w t -> p (a w t)"),
            )

        def quantise_w2_dealt(a):
            grouped = held([P, PACK, P, PACK], BF16, f"w2_grouped{a}")
            nc.scalar.activation(
                grouped[:].rearrange("p t m j -> p m j t"), w2_late[a][:].rearrange("p j (m t) -> p m j t", t=PACK), ACT.Copy
            )
            nc.vector.quantize_mx(w2_w_dealt[a][:].bitcast(FP8X4), w2_s_dealt[a][:], grouped[:].rearrange("p t m j -> p (t m j)"))

        def entries(idx, first, count):
            return idx[:, first // PER_COL : (first + count) // PER_COL]

        def gather_words(a, first, count):
            nc.vector.tensor_copy(v_w[a][:, first : first + count], tab_w[a][:].bitcast(U32).indirect(entries(idx1, first, count)))

        def stationary(c, a):
            if c < PACK:
                piece, first = divmod(c * P, PIECE)
                cols = slice(first, first + P)
                part, w2_cols = (0, cols) if piece == 0 else (c, slice(0, P))
                return (
                    w2_w[part][:, a, w2_cols], w2_s[part][:, a, w2_cols],
                    w1_early[:, a, 2 * c * P : 2 * (c + 1) * P], w1_s[:, a, c * P : (c + 1) * P],
                )
            t = c - PACK
            cols = slice(t * P, (t + 1) * P)
            return w2_w_dealt[a][:, cols], w2_s_dealt[a][:, cols], w1_dealt[:, a, t, :].bitcast(U8), w1_s_dealt[:, a, t, :]

        def make_h(c, first, count, number, values):
            acc = bank_tile(number)
            cols = slice(first, first + count)
            squares, table = [], []
            for a in range(PASSES):
                w2_codes, w2_scales, w1_codes, w1_scale_bytes = stationary(c, a)
                squares.append((w2_codes.bitcast(FP8X4), w2_scales, sq_w[a][:, cols].bitcast(FP8X4), sq_s[a][:, cols]))
                table.append((w1_codes.bitcast(FP4X4), w1_scale_bytes, v_w[a][:, cols].bitcast(FP8X4), v_s[a][:, cols]))
            passes = squares + table if first == 0 and c < 2 else table + squares
            for n, operands in enumerate(passes):
                nc.tensor.matmul_mx(acc[:, :count], *operands, start=(n == 0), stop=(n == len(passes) - 1))
            nc.scalar.activation(values, acc[:, :count], ACT.Tanh)

        def scatter_h(c, first, count, values):
            cols = slice(first, first + count)
            factor = weights[:, cols] if c < PACK else weights_dealt[c - PACK][:, cols]
            nc.vector.tensor_tensor(pages[c % PAGES][:].indirect(entries(idx2, first, count)), values, factor, MULT)

        def gain_plus_disp(c, gd):
            bias = gain_early[:, c : c + 1] if c < PACK else gain_dealt[:, c - PACK : c - PACK + 1]
            nc.scalar.activation(gd[:], d[c], ACT.Identity, bias=bias, scale=1.0)
            return gd

        def gather_rows(c, y, gd, first, count):
            nc.vector.tensor_tensor(y, pages[c % PAGES][:].indirect(entries(idx3, first, count)), gd[:, first : first + count], MULT)

        def turn(bank, place, term, start, stop):
            nc.tensor.matmul(bank[:, place * P : (place + 1) * P], term, ident[:], is_transpose=True, start=start, stop=stop)

        def turn_tile(c, y, zt, banks):
            for half in range(2):
                bank = bank_tile(banks[half])
                for n, term in enumerate((d[c], y)):
                    for k in range(4):
                        first = half * BANK + k * P
                        turn(bank, k, term[:, first : first + P], n == 0 and k == 0, n == 1 and k == 3)
                nc.scalar.copy(
                    zt[half][:, :, :, 32 * c : 32 * (c + 1), :], bank[:].rearrange("m (k p u e) -> m k u p e", p=32, u=2, e=2)
                )

        def quantise_z0(half, zt, codes):
            words = placed([P, BANK, 2], F32, f"z0_words{half}", 16 + 4 * half)
            for n, number in enumerate((4, 5)):
                bank = bank_tile(number)
                turned = bank[:].rearrange("p (k u m) -> p k u m", u=2, m=P)
                for k in range(2):
                    for u in range(2):
                        nc.tensor.transpose(
                            turned[:, k, u, :], zt[:, 2 * n + k, u, :, :].rearrange("m p e -> m (p e)").bitcast(F32), ident[:]
                        )
                nc.scalar.copy(
                    words[:, n * PIECE : (n + 1) * PIECE, :].rearrange("p (k m) u -> p k m u", m=P), turned.rearrange("p k u m -> p k m u")
                )
            cols = slice(half * BANK, (half + 1) * BANK)
            nc.vector.quantize_mx(codes[:, cols].bitcast(FP8X4), z_s[0][:, cols], words[:].rearrange("p m u -> p (m u)").bitcast(BF16))

        def out_pass(a, i, half, acc):
            first, count = TAIL_PARTS[i]
            cols = slice(first, first + count)
            tiles = BANK // count
            for k in range(tiles):
                n0 = (tiles * half + k) * P
                nc.tensor.matmul_mx(
                    acc[:, k * count : (k + 1) * count],
                    w3_w[:, a, n0 : n0 + P].bitcast(FP8X4), w3_s[:, a, n0 : n0 + P],
                    z_w[a, i].bitcast(FP8X4), z_s[a][:, cols],
                    start=(a == 0 and k == 0), stop=(a == 1 and k == tiles - 1),
                )

        ident = held([P, P], F32, "tab_s")
        make_identity(nc, ident[:])
        quantise_sq(0)
        quantise_w2(0)
        nc.vector.tensor_copy(w1_s_dealt[:], w1_s[:, :, K_PASS:].rearrange("p a (m t) -> p a t m", t=PACK))
        gather_words(0, 0, S)
        gather_words(1, 0, PIECE)

        def head_piece(c, piece, values):
            make_h(c, piece * PIECE, PIECE, (PAGES * piece + c) % 4, values)
            scatter_h(c, piece * PIECE, PIECE, values)

        def piece_of(c, piece):
            return h[c][:, piece * PIECE : (piece + 1) * PIECE]

        def spent(name):
            return held([P, PIECE], F32, name)[:]

        head_piece(0, 0, piece_of(0, 0))
        gather_words(1, PIECE, S - PIECE)
        middle = {1: 50, 2: 58, 3: 34}
        h.update({c: placed([P, S], F32, f"h{c}", middle[c]) for c in (1, 2)})
        quantise_w2(2)
        head_piece(1, 0, spent("w2_last"))
        for piece in (1, 2, 3):
            quantise_sq(piece)
            head_piece(2, piece - 1, spent(f"xn_last{piece}"))
            for c in range(2):
                head_piece(c, piece, piece_of(c, piece))
        head_piece(2, 3, piece_of(2, 3))

        def make_h_tile(c, values):
            h[c] = values
            for half in range(2):
                make_h(c, half * BANK, BANK, 6 + half, values[:, half * BANK : (half + 1) * BANK])

        gd = {0: gain_plus_disp(0, held([P, M], F32, "gd0"))}
        quantise_w2(3)
        quantise_w2_dealt(0)
        gd[1] = gain_plus_disp(1, held([P, M], F32, "gd1"))
        quantise_w2_dealt(1)
        make_h_tile(3, placed([P, S], F32, "h3", middle[3]))
        nc.scalar.copy(w1_dealt[:], w1_late[:].rearrange("p a (m t) -> p a t m", t=PACK))

        zt = [placed([P, 4, 2, P, 2], BF16, f"zt{half}", 28 - 4 * half) for half in range(2)]
        for c in range(PACK):
            gather_rows(c, h[c][:], gd[c], 0, M)
            turn_tile(c, h[c][:], zt, (2 * (c % 2), 2 * (c % 2) + 1))
            if c > 0:
                scatter_h(c + 2, 0, S, h[c + 2][:])
                gd[c + 1] = gain_plus_disp(c + 1, placed([P, M], F32, f"gd{c + 1}", middle[c] + (2 if c == 3 else -2)))
                make_h_tile(c + 3, placed([P, S], F32, f"h{c + 3}", middle[c] + (-2 if c == 3 else 2)))

        sums = [bank_tile(i) for i in range(PIECES)]

        def turn_pair(e, term, opens, closes):
            for i in range(PIECES):
                for k in range(2):
                    first = i * PIECE + k * P
                    turn(sums[i], 2 * k + e, term[:, first : first + P], opens and k == 0, closes and k == 1)

        turn_pair(0, d[4], True, False)
        turn_pair(1, d[5], False, False)
        gather_rows(4, h[4][:], gd[4], 0, M)
        turn_pair(0, h[4][:], False, False)
        scatter_h(6, 0, S, h[6][:])
        gd[5] = gain_plus_disp(5, placed([P, M], F32, "gd5", middle[1] + 2))
        codes0 = placed([P, M], U32, "codes0", middle[2] + 2)
        for half in range(2):
            quantise_z0(half, zt[half], codes0)
        for i, (first, count) in enumerate(TAIL_PARTS):
            z_w[0, i] = codes0[:, first : first + count]
        y5 = held([P, M], F32, "h0")
        gather_rows(5, y5[:], gd[5], 0, M)
        gd[6] = gain_plus_disp(6, placed([P, M], F32, "gd6", 40))
        make_h_tile(7, placed([P, S], F32, "h7", 44))
        gd[7] = gain_plus_disp(7, held([P, M], F32, "gd1"))
        turn_pair(1, y5[:], False, True)
        y_pair = {i: held([P, 2, TAIL_PARTS[i][1]], F32, f"xn_last{i + 1}") for i in range(PUT_OFF_FROM)}
        for i in range(PUT_OFF_FROM):
            gather_rows(6, y_pair[i][:, 0, :], gd[6], *TAIL_PARTS[i])
        scatter_h(7, 0, S, h[7][:])

        woven = [held([P, count, 2], F32, name) for (first, count), name in zip(TAIL_PARTS, ("d0", "d1", "d2", "d3", "gd0"))]
        turned_pair = []
        for i in range(PIECES):
            turned_pair.append(held([P, 2, P, 2], BF16, f"turned_pair{i}"))
            nc.scalar.copy(turned_pair[i][:], sums[i][:].rearrange("m (k e p) -> m k p e", k=2, e=2))
        for n in range(2):
            bank = bank_tile(4 + n)
            for place in range(4):
                i, k = 2 * n + place // 2, place % 2
                nc.tensor.transpose(
                    bank[:, place * P : (place + 1) * P], turned_pair[i][:, k, :, :].rearrange("m p e -> m (p e)").bitcast(F32), ident[:]
                )
            for i, (first, count) in enumerate(TAIL_PARTS):
                lo, hi = max(first, n * BANK), min(first + count, (n + 1) * BANK)
                if lo < hi:
                    nc.scalar.copy(woven[i][:, lo - first : hi - first, 0], bank[:, lo - n * BANK : hi - n * BANK])
        accs = {}
        for i, (first, count) in enumerate(TAIL_PARTS):
            for half in range(count // P):
                accs[i, half] = bank_tile((6 + first // P + half) % 8)
                out_pass(0, i, half, accs[i, half])

        def pair_sum(i):
            first, count = TAIL_PARTS[i]
            nc.vector.tensor_tensor(
                woven[i][:].bitcast(BF16)[:, :, 2:4].rearrange("p (c i) e -> p c e i", i=4),
                y_pair[i][:].rearrange("p e (c i) -> p c e i", i=4),
                d_pair[1][:, :, first : first + count].rearrange("p e (c i) -> p c e i", i=4),
                ADD,
            )

        def tail_codes(i):
            first, count = TAIL_PARTS[i]
            codes = held([P, count], U32, f"z_w1_{i}")
            z_w[1, i] = codes[:]
            nc.vector.quantize_mx(
                codes[:].bitcast(FP8X4), z_s[1][:, first : first + count], woven[i][:].rearrange("p m u -> p (m u)").bitcast(BF16)
            )

        def finish_out(i, half):
            first, count = TAIL_PARTS[i]
            tiles = BANK // count
            staged = placed([P, BANK], F32, f"staged{i}_{half}", 16 + 2 * (first // P + half))
            out_rows = out[:, first : first + count].rearrange("(k p) m -> p k m", p=P)
            out_pass(1, i, half, accs[i, half])
            copy = nc.vector.tensor_copy if (i, half) == (3, 1) else nc.scalar.copy
            copy(staged[:], accs[i, half][:])
            nc.sync.dma_start(out_rows[:, tiles * half : tiles * (half + 1), :], staged[:].rearrange("p (k m) -> p k m", k=tiles))

        def sum_and_weave(i):
            if i >= PUT_OFF_FROM:
                y_pair[i] = held([P, 2, TAIL_PARTS[i][1]], F32, f"xn_last{i % 2 + 1}")
                for c in (7, 6):
                    gather_rows(c, y_pair[i][:, c - 6, :], gd[c], *TAIL_PARTS[i])
            pair_sum(i)

        for i in range(PUT_OFF_FROM):
            gather_rows(7, y_pair[i][:, 1, :], gd[7], *TAIL_PARTS[i])
        sum_and_weave(0)
        for i, (first, count) in enumerate(TAIL_PARTS):
            if i < 1:
                sum_and_weave(i + 1)
            tail_codes(i)
            finish_out(i, 0)
            if 1 <= i < len(TAIL_PARTS) - 1:
                sum_and_weave(i + 1)
                finish_out(i, 1)
